import numpy as np
import ml_dtypes


def mxq(x, axis, fmt="e4m3"):
    dtype, down = {"e4m3": (ml_dtypes.float8_e4m3fn, 7), "e5m2": (ml_dtypes.float8_e5m2, 14)}[fmt]
    v = np.moveaxis(np.asarray(x, np.float32).astype(ml_dtypes.bfloat16).astype(np.float64), axis, -1)
    blocks = v.reshape(v.shape[:-1] + (-1, 32))
    amax = np.abs(blocks).max(-1, keepdims=True)
    byte = np.maximum(np.where(amax > 0, np.frexp(amax)[1] - 1 + 127, 0) - down, 1)
    scale = np.exp2(byte - 127.0)
    codes = (blocks / scale).astype(np.float32).astype(dtype).astype(np.float64)
    return np.moveaxis((codes * scale).reshape(v.shape), -1, axis)


WIDE = False


def mx_kscale(k):
    if not WIDE:
        return np.ones(k)
    levels = np.array([30, -30])
    if k % 512:
        return np.exp2(np.random.permutation(np.resize(levels, k // 32))).repeat(32)
    a = np.empty((k // 512, 16))
    for p in range(k // 512):
        a[p, :8] = np.random.permutation(np.resize(levels, 8))
        for g in range(8):
            far = levels[np.abs(levels - a[p, g]) >= 10]
            a[p, g + 8] = far[np.random.randint(len(far))]
    return np.exp2(a.ravel()).repeat(32)


def f64(x):
    return np.asarray(x).astype(np.float64)


E2M1 = np.array([0.0, 0.5, 1.0, 1.5, 2.0, 3.0, 4.0, 6.0, -0.0, -0.5, -1.0, -1.5, -2.0, -3.0, -4.0, -6.0])


def pack_weight(w, fmt):
    k, n = w.shape
    w = f64(np.asarray(w, np.float32).astype(ml_dtypes.bfloat16)).reshape(k // 32, 32, n)
    amax = np.abs(w).max(1)
    if fmt == "e4m3":
        byte = np.frexp(amax)[1] - 1 + 127 - 7
    else:
        mant, ex = np.frexp(amax / 6.0)
        byte = np.where(mant > 0.5, ex, ex - 1) + 127
    byte = np.clip(np.where(amax > 0, byte, 1), 1, 254)
    scaled = (w * np.exp2(127.0 - byte)[:, None, :]).reshape(k, n).astype(np.float32)
    by_word = np.ascontiguousarray(scaled.reshape(k // 512, 128, 4, n).transpose(0, 1, 3, 2))
    if fmt == "e4m3":
        words = by_word.astype(ml_dtypes.float8_e4m3fn).view(np.uint8)
    else:
        c = by_word.astype(ml_dtypes.float4_e2m1fn).view(np.uint8) & 0xF
        words = (c[..., 0::2] | (c[..., 1::2] << 4)).reshape(k // 512, 128, 2 * n)
    return np.ascontiguousarray(words), np.ascontiguousarray(byte.astype(np.uint8).reshape(k // 512, 16, n))


def unpack_weight(words, scales, fmt):
    g, _, n = scales.shape
    words = np.ascontiguousarray(words).reshape(g, 128, n, -1)
    if fmt == "e4m3":
        vals = words.view(ml_dtypes.float8_e4m3fn).astype(np.float64)
    else:
        nib = np.empty((g, 128, n, 4), np.uint8)
        nib[..., 0::2] = words & 0xF
        nib[..., 1::2] = words >> 4
        vals = E2M1[nib]
    vals = vals * np.repeat(np.exp2(scales.astype(np.float64) - 127.0), 8, axis=1)[..., None]
    return vals.transpose(0, 1, 3, 2).reshape(g * 512, n)


O, T, D, H = 512, 1536, 512, 1024


def setup_inputs():
    n = np.random.standard_normal
    s = mx_kscale(T)[:, None]
    m = np.exp(0.5 * n((T, 1)))
    x = n((T, D)) * s
    p_x4 = pack_weight(x[:O], "e2m1")
    return {
        "x4_words": p_x4[0],
        "x4_scales": p_x4[1],
        "x8": (x[O:]).astype(np.float32),
        "dy": (m * n((T, H)) / np.sqrt(T) / s).astype(np.float32),
    }


def reference(x4_words, x4_scales, x8, dy):
    x4_ = unpack_weight(x4_words, x4_scales, "e2m1")
    x8_ = mxq(f64(x8), 0, "e4m3")
    dy_ = mxq(f64(dy), 0, "e5m2")
    y = x4_.T @ dy_[:O] + x8_.T @ dy_[O:]
    return y

@@ -1,0 +1,159 @@
+from contextlib import ExitStack
+
+import concourse.mybir as mybir
+
+F32 = mybir.dt.float32
+BF16 = mybir.dt.bfloat16
+I32 = mybir.dt.int32
+U32 = mybir.dt.uint32
+U8 = mybir.dt.uint8
+E4M3X4 = mybir.dt.float8_e4m3fn_x4
+E5M2X4 = mybir.dt.float8_e5m2_x4
+E2M1X4 = mybir.dt.float4_e2m1fn_x4
+
+T, D, H = 1536, 512, 1024
+P = 128
+PACK = 4
+K_PASS = P * PACK
+M_TILE = 128
+N_TILE = 512
+M_TILES = D // M_TILE
+
+FLOPS = 2 * T * D * H
+
+
+HALF = N_TILE // 2
+
+
+def tile_mix_dwsav_none_kernel(tc, x4_words, x4_scales, x8, dy, out):
+    nc = tc.nc
+    with ExitStack() as ctx:
+        keep = ctx.enter_context(tc.tile_pool(name="keep", bufs=1))
+        psum = ctx.enter_context(tc.psum_pool(name="psum", bufs=1))
+        ctx.enter_context(tc.manual_schedule())
+
+        x4_codes = keep.tile([P, 2 * D], U8, name="x4_codes", align_bytes=64)
+        x4_plane = keep.tile([P, D], U8, name="x4_plane", align_bytes=64)
+        nc.vector.memset(x4_plane[:].bitcast(I32), 0)
+
+        def load(name, src, row0, cols):
+            raw = keep.tile([P, PACK, cols.stop - cols.start], F32, name="raw_" + name, align_bytes=64)
+            rows = src[row0 : row0 + K_PASS, cols]
+            nc.sync.dma_start(out=raw[:], in_=rows.rearrange("(p j) w -> p j w", j=PACK))
+            return raw
+
+        def load_dy(a, lo, hi):
+            return load("dy%d_%d" % (a, lo), dy, a * K_PASS, slice(lo, hi))
+
+        def load_x8(a):
+            return load("x8_%d" % a, x8, (a - 1) * K_PASS, slice(0, D))
+
+        dy00 = load_dy(0, 0, N_TILE)
+        nc.sync.dma_start(out=x4_codes[:].bitcast(I32), in_=x4_words[0].bitcast(I32))
+        for q in range(4):
+            nc.sync.dma_start(
+                out=x4_plane[32 * q : 32 * q + 4, :].bitcast(I32),
+                in_=x4_scales[0, 4 * q : 4 * q + 4, :].bitcast(I32),
+            )
+        x81 = load_x8(1)
+        dy10 = load_dy(1, 0, N_TILE)
+        x82 = load_x8(2)
+        dy20 = load_dy(2, 0, N_TILE)
+        dy01 = load_dy(0, N_TILE, H)
+        dy11 = load_dy(1, N_TILE, H)
+        dy21a = load_dy(2, N_TILE, H - 128)
+        dy21b = load_dy(2, H - 128, H)
+
+        acc = {}
+        for n in range(2):
+            for m in range(M_TILES):
+                acc[m, n] = psum.tile([M_TILE, N_TILE], F32, name="acc_%d%d" % (m, n))
+
+        def operand(name):
+            grouped = keep.tile([P, PACK * N_TILE], BF16, name="grouped_" + name, align_bytes=64)
+            codes = keep.tile([P, N_TILE], U32, name="codes_" + name, align_bytes=64)
+            plane = keep.tile([P, N_TILE], U8, name="plane_" + name, align_bytes=64)
+            return grouped, codes, plane
+
+        def interleave(copy, raw, lo, op, at, width):
+            copy(
+                out=op[0][:, PACK * at : PACK * (at + width)].rearrange("p (c i j) -> p c j i", i=4, j=PACK),
+                in_=raw[:, :, lo : lo + width].rearrange("p j (c i) -> p c j i", i=4),
+            )
+
+        def quantize(op, fmt, at, width):
+            nc.vector.quantize_mx(
+                out=op[1][:, at : at + width].bitcast(fmt),
+                scales=op[2][:, at : at + width],
+                in_=op[0][:, PACK * at : PACK * (at + width)],
+            )
+
+        def whole(name, raw, fmt, v_cols):
+            op = operand(name)
+            interleave(nc.vector.tensor_copy, raw, 0, op, 0, v_cols)
+            interleave(nc.scalar.copy, raw, v_cols, op, v_cols, N_TILE - v_cols)
+            quantize(op, fmt, 0, N_TILE)
+            return op
+
+        def in_halves(name, raw, fmt):
+            op = operand(name)
+            interleave(nc.vector.tensor_copy, raw, 0, op, 0, HALF)
+            interleave(nc.scalar.copy, raw, HALF, op, HALF, HALF)
+            quantize(op, fmt, 0, HALF)
+            quantize(op, fmt, HALF, HALF)
+            return op
+
+        def multiply(a, n, stationary, moving):
+            for m in range(M_TILES):
+                cols = slice(m * M_TILE, (m + 1) * M_TILE)
+                if a == 0:
+                    lhsT = x4_codes[:, 2 * m * M_TILE : 2 * (m + 1) * M_TILE].bitcast(E2M1X4)
+                    lhsT_scale = x4_plane[:, cols]
+                else:
+                    lhsT = stationary[1][:, cols].bitcast(E4M3X4)
+                    lhsT_scale = stationary[2][:, cols]
+                nc.tensor.matmul_mx(
+                    out=acc[m, n][:],
+                    lhsT=lhsT,
+                    lhsT_scale=lhsT_scale,
+                    rhs=moving[1][:].bitcast(E5M2X4),
+                    rhs_scale=moving[2][:],
+                    start=(a == 0),
+                    stop=(a == 2),
+                )
+
+        multiply(0, 0, None, whole("dy00", dy00, E5M2X4, 288))
+        s1 = whole("x81", x81, E4M3X4, 288)
+        multiply(1, 0, s1, whole("dy10", dy10, E5M2X4, 288))
+        s2 = whole("x82", x82, E4M3X4, 288)
+        multiply(2, 0, s2, whole("dy20", dy20, E5M2X4, 288))
+        multiply(0, 1, None, whole("dy01", dy01, E5M2X4, 352))
+        left = keep.tile([M_TILE, M_TILES, N_TILE], F32, name="left", align_bytes=64)
+        for m in range(M_TILES):
+            copy = nc.vector.tensor_copy if m % 2 == 0 else nc.scalar.copy
+            copy(out=left[:, m, :], in_=acc[m, 0][:])
+        nc.sync.dma_start(out=out[:, 0:N_TILE].rearrange("(m p) h -> p m h", p=M_TILE), in_=left[:])
+
+        op11 = in_halves("dy11", dy11, E5M2X4)
+        multiply(1, 1, s1, op11)
+        op21 = operand("dy21")
+        interleave(nc.vector.tensor_copy, dy21a, 0, op21, 0, 256)
+        interleave(nc.scalar.copy, dy21a, 256, op21, 256, 128)
+        quantize(op21, E5M2X4, 0, 256)
+        quantize(op21, E5M2X4, 256, 128)
+        interleave(nc.scalar.copy, dy21b, 0, op21, 384, 128)
+        quantize(op21, E5M2X4, 384, 128)
+        multiply(2, 1, s2, op21)
+        for m in range(M_TILES):
+            right = keep.tile([M_TILE, N_TILE], F32, name="right_%d" % m, align_bytes=64)
+            copy = nc.vector.tensor_copy if m % 2 == 0 else nc.scalar.copy
+            queue = nc.sync
+            parts = 2 if m == 0 else 1
+            width = N_TILE // parts
+            for part in range(parts):
+                cols = slice(part * width, (part + 1) * width)
+                copy(out=right[:, cols], in_=acc[m, 1][:, cols])
+                queue.dma_start(
+                    out=out[m * M_TILE : (m + 1) * M_TILE, N_TILE + cols.start : N_TILE + cols.stop],
+                    in_=right[:, cols],
+                )

@@ -21,8 +21,7 @@ M_TILES = D // M_TILE
 
 FLOPS = 2 * T * D * H
 
-
-HALF = N_TILE // 2
+H_TILES = H // N_TILE
 
 
 def tile_mix_dwsav_none_kernel(tc, x4_words, x4_scales, x8, dy, out):
@@ -31,43 +30,36 @@ def tile_mix_dwsav_none_kernel(tc, x4_words, x4_scales, x8, dy, out):
         keep = ctx.enter_context(tc.tile_pool(name="keep", bufs=1))
         psum = ctx.enter_context(tc.psum_pool(name="psum", bufs=1))
         ctx.enter_context(tc.manual_schedule())
+        vector, scalar = nc.vector.tensor_copy, nc.scalar.copy
 
         x4_codes = keep.tile([P, 2 * D], U8, name="x4_codes", align_bytes=64)
         x4_plane = keep.tile([P, D], U8, name="x4_plane", align_bytes=64)
         nc.vector.memset(x4_plane[:].bitcast(I32), 0)
 
-        def load(name, src, row0, cols):
-            raw = keep.tile([P, PACK, cols.stop - cols.start], F32, name="raw_" + name, align_bytes=64)
-            rows = src[row0 : row0 + K_PASS, cols]
+        def load(name, src, row0, lo, hi):
+            raw = keep.tile([P, PACK, hi - lo], F32, name="raw_" + name, align_bytes=64)
+            rows = src[row0 : row0 + K_PASS, lo:hi]
             nc.sync.dma_start(out=raw[:], in_=rows.rearrange("(p j) w -> p j w", j=PACK))
             return raw
 
         def load_dy(a, lo, hi):
-            return load("dy%d_%d" % (a, lo), dy, a * K_PASS, slice(lo, hi))
+            return load("dy%d_%d" % (a, lo), dy, a * K_PASS, lo, hi)
 
-        def load_x8(a):
-            return load("x8_%d" % a, x8, (a - 1) * K_PASS, slice(0, D))
+        def load_x8(a, lo, hi):
+            return load("x8_%d_%d" % (a, lo), x8, (a - 1) * K_PASS, lo, hi)
 
-        dy00 = load_dy(0, 0, N_TILE)
-        nc.sync.dma_start(out=x4_codes[:].bitcast(I32), in_=x4_words[0].bitcast(I32))
-        for q in range(4):
+        def load_x4_codes(lo, hi):
             nc.sync.dma_start(
-                out=x4_plane[32 * q : 32 * q + 4, :].bitcast(I32),
-                in_=x4_scales[0, 4 * q : 4 * q + 4, :].bitcast(I32),
+                out=x4_codes[:, 2 * lo : 2 * hi].bitcast(I32),
+                in_=x4_words[0, :, 2 * lo : 2 * hi].bitcast(I32),
             )
-        x81 = load_x8(1)
-        dy10 = load_dy(1, 0, N_TILE)
-        x82 = load_x8(2)
-        dy20 = load_dy(2, 0, N_TILE)
-        dy01 = load_dy(0, N_TILE, H)
-        dy11 = load_dy(1, N_TILE, H)
-        dy21a = load_dy(2, N_TILE, H - 128)
-        dy21b = load_dy(2, H - 128, H)
 
-        acc = {}
-        for n in range(2):
-            for m in range(M_TILES):
-                acc[m, n] = psum.tile([M_TILE, N_TILE], F32, name="acc_%d%d" % (m, n))
+        def load_x4_scales():
+            for q in range(4):
+                nc.sync.dma_start(
+                    out=x4_plane[32 * q : 32 * q + 4, :].bitcast(I32),
+                    in_=x4_scales[0, 4 * q : 4 * q + 4, :].bitcast(I32),
+                )
 
         def operand(name):
             grouped = keep.tile([P, PACK * N_TILE], BF16, name="grouped_" + name, align_bytes=64)
@@ -75,11 +67,28 @@ def tile_mix_dwsav_none_kernel(tc, x4_words, x4_scales, x8, dy, out):
             plane = keep.tile([P, N_TILE], U8, name="plane_" + name, align_bytes=64)
             return grouped, codes, plane
 
+        acc, moving, stationary, rows = {}, {}, {}, {}
+        for m in range(M_TILES):
+            rows[m] = keep.tile([M_TILE, H], F32, name="rows_%d" % m, align_bytes=64)
+            for n in range(H_TILES):
+                acc[m, n] = psum.tile([M_TILE, N_TILE], F32, name="acc_%d%d" % (m, n))
+        for a in range(3):
+            for n in range(H_TILES):
+                moving[a, n] = operand("dy%d%d" % (a, n))
+        for a in (1, 2):
+            stationary[a] = operand("x8_%d" % a)
+
         def interleave(copy, raw, lo, op, at, width):
             copy(
                 out=op[0][:, PACK * at : PACK * (at + width)].rearrange("p (c i j) -> p c j i", i=4, j=PACK),
                 in_=raw[:, :, lo : lo + width].rearrange("p j (c i) -> p c j i", i=4),
             )
+
+        def shared(raw, lo, op, at, width, v_cols):
+            if v_cols > 0:
+                interleave(vector, raw, lo, op, at, v_cols)
+            if v_cols < width:
+                interleave(scalar, raw, lo + v_cols, op, at + v_cols, width - v_cols)
 
         def quantize(op, fmt, at, width):
             nc.vector.quantize_mx(
@@ -88,72 +97,89 @@ def tile_mix_dwsav_none_kernel(tc, x4_words, x4_scales, x8, dy, out):
                 in_=op[0][:, PACK * at : PACK * (at + width)],
             )
 
-        def whole(name, raw, fmt, v_cols):
-            op = operand(name)
-            interleave(nc.vector.tensor_copy, raw, 0, op, 0, v_cols)
-            interleave(nc.scalar.copy, raw, v_cols, op, v_cols, N_TILE - v_cols)
-            quantize(op, fmt, 0, N_TILE)
-            return op
+        def quantize_dy(a, n, at=0, width=N_TILE):
+            quantize(moving[a, n], E5M2X4, at, width)
 
-        def in_halves(name, raw, fmt):
-            op = operand(name)
-            interleave(nc.vector.tensor_copy, raw, 0, op, 0, HALF)
-            interleave(nc.scalar.copy, raw, HALF, op, HALF, HALF)
-            quantize(op, fmt, 0, HALF)
-            quantize(op, fmt, HALF, HALF)
-            return op
+        def quantize_x8(a, at=0, width=D):
+            quantize(stationary[a], E4M3X4, at, width)
 
-        def multiply(a, n, stationary, moving):
+        passes_done = {}
+
+        def multiply(a, m, n):
+            cols = slice(m * M_TILE, (m + 1) * M_TILE)
+            if a == 0:
+                lhsT = x4_codes[:, 2 * m * M_TILE : 2 * (m + 1) * M_TILE].bitcast(E2M1X4)
+                lhsT_scale = x4_plane[:, cols]
+            else:
+                lhsT = stationary[a][1][:, cols].bitcast(E4M3X4)
+                lhsT_scale = stationary[a][2][:, cols]
+            done = passes_done.get((m, n), 0)
+            nc.tensor.matmul_mx(
+                out=acc[m, n][:],
+                lhsT=lhsT,
+                lhsT_scale=lhsT_scale,
+                rhs=moving[a, n][1][:].bitcast(E5M2X4),
+                rhs_scale=moving[a, n][2][:],
+                start=(done == 0),
+                stop=(done == 2),
+            )
+            passes_done[m, n] = done + 1
+
+        def drain(copy, m, n, lo=0, hi=N_TILE):
+            copy(out=rows[m][:, n * N_TILE + lo : n * N_TILE + hi], in_=acc[m, n][:, lo:hi])
+
+        def store(m, lo, hi):
+            nc.sync.dma_start(out=out[m * M_TILE : (m + 1) * M_TILE, lo:hi], in_=rows[m][:, lo:hi])
+
+        dy0 = load_dy(0, 0, H)
+        load_x4_scales()
+        x1 = load_x8(1, 0, D)
+        x2 = load_x8(2, 0, D)
+        dy10 = load_dy(1, 0, N_TILE)
+        load_x4_codes(0, D)
+        dy20 = load_dy(2, 0, N_TILE)
+        dy11 = load_dy(1, N_TILE, H)
+        dy21a = load_dy(2, N_TILE, 896)
+        dy21b = load_dy(2, 896, H)
+
+        for n in range(H_TILES):
+            shared(dy0, n * N_TILE, moving[0, n], 0, N_TILE, 288)
+        for n in range(H_TILES):
+            quantize_dy(0, n)
+        for a, raw in ((1, x1), (2, x2)):
+            shared(raw, 0, stationary[a], 0, D, 288)
+            quantize_x8(a)
+        for m in range(M_TILES):
+            multiply(0, m, 0)
+        for a, raw in ((1, dy10), (2, dy20)):
+            shared(raw, 0, moving[a, 0], 0, N_TILE, 320)
+            quantize_dy(a, 0)
             for m in range(M_TILES):
-                cols = slice(m * M_TILE, (m + 1) * M_TILE)
-                if a == 0:
-                    lhsT = x4_codes[:, 2 * m * M_TILE : 2 * (m + 1) * M_TILE].bitcast(E2M1X4)
-                    lhsT_scale = x4_plane[:, cols]
-                else:
-                    lhsT = stationary[1][:, cols].bitcast(E4M3X4)
-                    lhsT_scale = stationary[2][:, cols]
-                nc.tensor.matmul_mx(
-                    out=acc[m, n][:],
-                    lhsT=lhsT,
-                    lhsT_scale=lhsT_scale,
-                    rhs=moving[1][:].bitcast(E5M2X4),
-                    rhs_scale=moving[2][:],
-                    start=(a == 0),
-                    stop=(a == 2),
-                )
-
-        multiply(0, 0, None, whole("dy00", dy00, E5M2X4, 288))
-        s1 = whole("x81", x81, E4M3X4, 288)
-        multiply(1, 0, s1, whole("dy10", dy10, E5M2X4, 288))
-        s2 = whole("x82", x82, E4M3X4, 288)
-        multiply(2, 0, s2, whole("dy20", dy20, E5M2X4, 288))
-        multiply(0, 1, None, whole("dy01", dy01, E5M2X4, 352))
-        left = keep.tile([M_TILE, M_TILES, N_TILE], F32, name="left", align_bytes=64)
+                multiply(a, m, 0)
         for m in range(M_TILES):
-            copy = nc.vector.tensor_copy if m % 2 == 0 else nc.scalar.copy
-            copy(out=left[:, m, :], in_=acc[m, 0][:])
-        nc.sync.dma_start(out=out[:, 0:N_TILE].rearrange("(m p) h -> p m h", p=M_TILE), in_=left[:])
-
-        op11 = in_halves("dy11", dy11, E5M2X4)
-        multiply(1, 1, s1, op11)
-        op21 = operand("dy21")
-        interleave(nc.vector.tensor_copy, dy21a, 0, op21, 0, 256)
-        interleave(nc.scalar.copy, dy21a, 256, op21, 256, 128)
-        quantize(op21, E5M2X4, 0, 256)
-        quantize(op21, E5M2X4, 256, 128)
-        interleave(nc.scalar.copy, dy21b, 0, op21, 384, 128)
-        quantize(op21, E5M2X4, 384, 128)
-        multiply(2, 1, s2, op21)
+            multiply(0, m, 1)
+        drain(scalar, 0, 0)
+        store(0, 0, N_TILE)
+        shared(dy11, 0, moving[1, 1], 0, N_TILE, 448)
+        quantize_dy(1, 1)
         for m in range(M_TILES):
-            right = keep.tile([M_TILE, N_TILE], F32, name="right_%d" % m, align_bytes=64)
-            copy = nc.vector.tensor_copy if m % 2 == 0 else nc.scalar.copy
-            queue = nc.sync
+            multiply(1, m, 1)
+        drain(scalar, 1, 0)
+        store(1, 0, N_TILE)
+        drain(scalar, 2, 0)
+        store(2, 0, N_TILE)
+        shared(dy21a, 0, moving[2, 1], 0, 384, 256)
+        quantize_dy(2, 1, 0, 256)
+        shared(dy21b, 0, moving[2, 1], 384, 128, 0)
+        quantize_dy(2, 1, 256, 128)
+        quantize_dy(2, 1, 384, 128)
+        for m in range(M_TILES):
+            multiply(2, m, 1)
+        drain(scalar, 3, 0)
+        store(3, 0, N_TILE)
+        for m in range(M_TILES):
             parts = 2 if m == 0 else 1
             width = N_TILE // parts
             for part in range(parts):
-                cols = slice(part * width, (part + 1) * width)
-                copy(out=right[:, cols], in_=acc[m, 1][:, cols])
-                queue.dma_start(
-                    out=out[m * M_TILE : (m + 1) * M_TILE, N_TILE + cols.start : N_TILE + cols.stop],
-                    in_=right[:, cols],
-                )
+                drain(vector if m % 2 == 0 else scalar, m, 1, part * width, (part + 1) * width)
+                store(m, N_TILE + part * width, N_TILE + (part + 1) * width)

@@ -22,6 +22,7 @@ M_TILES = D // M_TILE
 FLOPS = 2 * T * D * H
 
 H_TILES = H // N_TILE
+HALF = N_TILE // 2
 
 
 def tile_mix_dwsav_none_kernel(tc, x4_words, x4_scales, x8, dy, out):
@@ -135,12 +136,18 @@ def tile_mix_dwsav_none_kernel(tc, x4_words, x4_scales, x8, dy, out):
         load_x4_scales()
         x1 = load_x8(1, 0, D)
         x2 = load_x8(2, 0, D)
-        dy10 = load_dy(1, 0, N_TILE)
         load_x4_codes(0, D)
+        dy10 = load_dy(1, 0, N_TILE)
         dy20 = load_dy(2, 0, N_TILE)
         dy11 = load_dy(1, N_TILE, H)
         dy21a = load_dy(2, N_TILE, 896)
         dy21b = load_dy(2, 896, H)
+
+        def in_halves(raw, a, n, v_cols):
+            interleave(vector, raw, 0, moving[a, n], 0, HALF)
+            shared(raw, HALF, moving[a, n], HALF, HALF, v_cols)
+            quantize_dy(a, n, 0, HALF)
+            quantize_dy(a, n, HALF, HALF)
 
         for n in range(H_TILES):
             shared(dy0, n * N_TILE, moving[0, n], 0, N_TILE, 288)
@@ -151,25 +158,27 @@ def tile_mix_dwsav_none_kernel(tc, x4_words, x4_scales, x8, dy, out):
             quantize_x8(a)
         for m in range(M_TILES):
             multiply(0, m, 0)
+        for m in (0, 1):
+            multiply(0, m, 1)
         for a, raw in ((1, dy10), (2, dy20)):
-            shared(raw, 0, moving[a, 0], 0, N_TILE, 320)
-            quantize_dy(a, 0)
+            in_halves(raw, a, 0, 64)
             for m in range(M_TILES):
                 multiply(a, m, 0)
-        for m in range(M_TILES):
+        for m in (2, 3):
             multiply(0, m, 1)
         drain(scalar, 0, 0)
         store(0, 0, N_TILE)
-        shared(dy11, 0, moving[1, 1], 0, N_TILE, 448)
-        quantize_dy(1, 1)
+        in_halves(dy11, 1, 1, 192)
         for m in range(M_TILES):
             multiply(1, m, 1)
         drain(scalar, 1, 0)
         store(1, 0, N_TILE)
         drain(scalar, 2, 0)
         store(2, 0, N_TILE)
-        shared(dy21a, 0, moving[2, 1], 0, 384, 256)
-        quantize_dy(2, 1, 0, 256)
+        interleave(vector, dy21a, 0, moving[2, 1], 0, 128)
+        shared(dy21a, 128, moving[2, 1], 128, 256, 128)
+        quantize_dy(2, 1, 0, 128)
+        quantize_dy(2, 1, 128, 128)
         shared(dy21b, 0, moving[2, 1], 384, 128, 0)
         quantize_dy(2, 1, 256, 128)
         quantize_dy(2, 1, 384, 128)

@@ -166,11 +166,12 @@ def tile_mix_dwsav_none_kernel(tc, x4_words, x4_scales, x8, dy, out):
                 multiply(a, m, 0)
         for m in (2, 3):
             multiply(0, m, 1)
-        drain(scalar, 0, 0)
-        store(0, 0, N_TILE)
+
         in_halves(dy11, 1, 1, 192)
         for m in range(M_TILES):
             multiply(1, m, 1)
+        drain(scalar, 0, 0)
+        store(0, 0, N_TILE)
         drain(scalar, 1, 0)
         store(1, 0, N_TILE)
         drain(scalar, 2, 0)

@@ -75,7 +75,18 @@ def tile_mix_dwsav_none_kernel(tc, x4_words, x4_scales, x8, dy, out):
                 acc[m, n] = psum.tile([M_TILE, N_TILE], F32, name="acc_%d%d" % (m, n))
         for a in range(3):
             for n in range(H_TILES):
-                moving[a, n] = operand("dy%d%d" % (a, n))
+                if (a, n) != (2, 1):
+                    moving[a, n] = operand("dy%d%d" % (a, n))
+        last = (
+            keep.tile([P, PACK * 3 * HALF], BF16, name="grouped_last", align_bytes=64),
+            keep.tile([P, 3 * HALF], U32, name="codes_last", align_bytes=64),
+            keep.tile([P, 3 * HALF], U8, name="plane_last", align_bytes=64),
+        )
+        nc.vector.memset(last[1][:, HALF : 2 * HALF].bitcast(I32), 0)
+        nc.vector.memset(last[2][:, HALF : 2 * HALF].bitcast(I32), 0)
+        partial = {}
+        for m in range(M_TILES):
+            partial[m] = keep.tile([M_TILE, HALF], F32, name="partial_%d" % m, align_bytes=64)
         for a in (1, 2):
             stationary[a] = operand("x8_%d" % a)
 
@@ -126,6 +137,26 @@ def tile_mix_dwsav_none_kernel(tc, x4_words, x4_scales, x8, dy, out):
             )
             passes_done[m, n] = done + 1
 
+        def multiply_last(m, at, into, start):
+            cols = slice(m * M_TILE, (m + 1) * M_TILE)
+            nc.tensor.matmul_mx(
+                out=into[:],
+                lhsT=stationary[2][1][:, cols].bitcast(E4M3X4),
+                lhsT_scale=stationary[2][2][:, cols],
+                rhs=last[1][:, at : at + N_TILE].bitcast(E5M2X4),
+                rhs_scale=last[2][:, at : at + N_TILE],
+                start=start,
+                stop=True,
+            )
+
+        def keep_partial(copy, m):
+            copy(out=partial[m][:], in_=acc[m, 1][:, HALF:])
+
+        def finish_late(m):
+            nc.vector.tensor_tensor(
+                out=rows[m][:, H - HALF :], in0=acc[m, 0][:, HALF:], in1=partial[m][:], op=mybir.AluOpType.add
+            )
+
         def drain(copy, m, n, lo=0, hi=N_TILE):
             copy(out=rows[m][:, n * N_TILE + lo : n * N_TILE + hi], in_=acc[m, n][:, lo:hi])
 
@@ -140,8 +171,8 @@ def tile_mix_dwsav_none_kernel(tc, x4_words, x4_scales, x8, dy, out):
         dy10 = load_dy(1, 0, N_TILE)
         dy20 = load_dy(2, 0, N_TILE)
         dy11 = load_dy(1, N_TILE, H)
-        dy21a = load_dy(2, N_TILE, 896)
-        dy21b = load_dy(2, 896, H)
+        dy21a = load_dy(2, N_TILE, H - HALF)
+        dy21b = load_dy(2, H - HALF, H)
 
         def in_halves(raw, a, n, v_cols):
             interleave(vector, raw, 0, moving[a, n], 0, HALF)
@@ -167,29 +198,31 @@ def tile_mix_dwsav_none_kernel(tc, x4_words, x4_scales, x8, dy, out):
         for m in (2, 3):
             multiply(0, m, 1)
 
-        in_halves(dy11, 1, 1, 192)
-        for m in range(M_TILES):
-            multiply(1, m, 1)
         drain(scalar, 0, 0)
         store(0, 0, N_TILE)
-        drain(scalar, 1, 0)
-        store(1, 0, N_TILE)
-        drain(scalar, 2, 0)
-        store(2, 0, N_TILE)
-        interleave(vector, dy21a, 0, moving[2, 1], 0, 128)
-        shared(dy21a, 128, moving[2, 1], 128, 256, 128)
-        quantize_dy(2, 1, 0, 128)
-        quantize_dy(2, 1, 128, 128)
-        shared(dy21b, 0, moving[2, 1], 384, 128, 0)
-        quantize_dy(2, 1, 256, 128)
-        quantize_dy(2, 1, 384, 128)
+        in_halves(dy11, 1, 1, 128)
         for m in range(M_TILES):
-            multiply(2, m, 1)
-        drain(scalar, 3, 0)
-        store(3, 0, N_TILE)
+            multiply(1, m, 1)
+        for m in range(1, M_TILES):
+            drain(scalar, m, 0)
+            store(m, 0, N_TILE)
+        interleave(vector, dy21a, 0, last, 0, 128)
+        interleave(vector, dy21a, 128, last, 128, 128)
+        quantize(last, E5M2X4, 0, 128)
+        quantize(last, E5M2X4, 128, 128)
         for m in range(M_TILES):
-            parts = 2 if m == 0 else 1
-            width = N_TILE // parts
-            for part in range(parts):
-                drain(vector if m % 2 == 0 else scalar, m, 1, part * width, (part + 1) * width)
-                store(m, N_TILE + part * width, N_TILE + (part + 1) * width)
+            multiply_last(m, 0, acc[m, 1], False)
+        interleave(vector, dy21b, 0, last, 2 * HALF, 128)
+        shared(dy21b, 128, last, 2 * HALF + 128, 128, 32)
+        quantize(last, E5M2X4, 2 * HALF, 128)
+        quantize(last, E5M2X4, 2 * HALF + 128, 128)
+        for m in range(M_TILES):
+            multiply_last(m, HALF, acc[m, 0], True)
+        for m in range(M_TILES):
+            copy = scalar if m % 2 == 0 else vector
+            drain(copy, m, 1, 0, HALF)
+            store(m, N_TILE, H - HALF)
+            keep_partial(vector if m == 1 else scalar, m)
+        for m in range(M_TILES):
+            finish_late(m)
+            store(m, H - HALF, H)

@@ -23,6 +23,17 @@ FLOPS = 2 * T * D * H
 
 H_TILES = H // N_TILE
 HALF = N_TILE // 2
+V20 = 64
+VS = [256, 256, 256, 256]
+BD = "ssss"
+BM = [2, 2]
+CM = [1, 1, 1, 1]
+PD = "s"
+QS = [[128, 128], [128, 128], [128, 128], [128, 64, 64]]
+E0 = 4
+PPOS = 0
+VA = 0
+PIPE = 0
 
 
 def tile_mix_dwsav_none_kernel(tc, x4_words, x4_scales, x8, dy, out):
@@ -62,33 +73,24 @@ def tile_mix_dwsav_none_kernel(tc, x4_words, x4_scales, x8, dy, out):
                     in_=x4_scales[0, 4 * q : 4 * q + 4, :].bitcast(I32),
                 )
 
-        def operand(name):
-            grouped = keep.tile([P, PACK * N_TILE], BF16, name="grouped_" + name, align_bytes=64)
-            codes = keep.tile([P, N_TILE], U32, name="codes_" + name, align_bytes=64)
-            plane = keep.tile([P, N_TILE], U8, name="plane_" + name, align_bytes=64)
+        def operand(name, width):
+            grouped = keep.tile([P, PACK * width], BF16, name="grouped_" + name, align_bytes=64)
+            codes = keep.tile([P, width], U32, name="codes_" + name, align_bytes=64)
+            plane = keep.tile([P, width], U8, name="plane_" + name, align_bytes=64)
             return grouped, codes, plane
 
-        acc, moving, stationary, rows = {}, {}, {}, {}
+        acc, moving, stationary = {}, {}, {}
+        left = keep.tile([M_TILE, M_TILES * N_TILE], F32, name="left", align_bytes=64)
+        mid = keep.tile([M_TILE, M_TILES * HALF], F32, name="mid", align_bytes=64)
+        right = keep.tile([M_TILE, M_TILES * HALF], F32, name="right", align_bytes=64)
+        partial = keep.tile([M_TILE, M_TILES * HALF], F32, name="partial", align_bytes=64)
         for m in range(M_TILES):
-            rows[m] = keep.tile([M_TILE, H], F32, name="rows_%d" % m, align_bytes=64)
             for n in range(H_TILES):
                 acc[m, n] = psum.tile([M_TILE, N_TILE], F32, name="acc_%d%d" % (m, n))
         for a in range(3):
-            for n in range(H_TILES):
-                if (a, n) != (2, 1):
-                    moving[a, n] = operand("dy%d%d" % (a, n))
-        last = (
-            keep.tile([P, PACK * 3 * HALF], BF16, name="grouped_last", align_bytes=64),
-            keep.tile([P, 3 * HALF], U32, name="codes_last", align_bytes=64),
-            keep.tile([P, 3 * HALF], U8, name="plane_last", align_bytes=64),
-        )
-        nc.vector.memset(last[1][:, HALF : 2 * HALF].bitcast(I32), 0)
-        nc.vector.memset(last[2][:, HALF : 2 * HALF].bitcast(I32), 0)
-        partial = {}
-        for m in range(M_TILES):
-            partial[m] = keep.tile([M_TILE, HALF], F32, name="partial_%d" % m, align_bytes=64)
+            moving[a] = operand("dy%d" % a, H)
         for a in (1, 2):
-            stationary[a] = operand("x8_%d" % a)
+            stationary[a] = operand("x8_%d" % a, D)
 
         def interleave(copy, raw, lo, op, at, width):
             copy(
@@ -109,15 +111,13 @@ def tile_mix_dwsav_none_kernel(tc, x4_words, x4_scales, x8, dy, out):
                 in_=op[0][:, PACK * at : PACK * (at + width)],
             )
 
-        def quantize_dy(a, n, at=0, width=N_TILE):
-            quantize(moving[a, n], E5M2X4, at, width)
+        def quantize_dy(a, at, width):
+            quantize(moving[a], E5M2X4, at, width)
 
         def quantize_x8(a, at=0, width=D):
             quantize(stationary[a], E4M3X4, at, width)
 
-        passes_done = {}
-
-        def multiply(a, m, n):
+        def multiply(a, m, bank, at, start, stop):
             cols = slice(m * M_TILE, (m + 1) * M_TILE)
             if a == 0:
                 lhsT = x4_codes[:, 2 * m * M_TILE : 2 * (m + 1) * M_TILE].bitcast(E2M1X4)
@@ -125,43 +125,24 @@ def tile_mix_dwsav_none_kernel(tc, x4_words, x4_scales, x8, dy, out):
             else:
                 lhsT = stationary[a][1][:, cols].bitcast(E4M3X4)
                 lhsT_scale = stationary[a][2][:, cols]
-            done = passes_done.get((m, n), 0)
             nc.tensor.matmul_mx(
-                out=acc[m, n][:],
+                out=acc[m, bank][:],
                 lhsT=lhsT,
                 lhsT_scale=lhsT_scale,
-                rhs=moving[a, n][1][:].bitcast(E5M2X4),
-                rhs_scale=moving[a, n][2][:],
-                start=(done == 0),
-                stop=(done == 2),
-            )
-            passes_done[m, n] = done + 1
-
-        def multiply_last(m, at, into, start):
-            cols = slice(m * M_TILE, (m + 1) * M_TILE)
-            nc.tensor.matmul_mx(
-                out=into[:],
-                lhsT=stationary[2][1][:, cols].bitcast(E4M3X4),
-                lhsT_scale=stationary[2][2][:, cols],
-                rhs=last[1][:, at : at + N_TILE].bitcast(E5M2X4),
-                rhs_scale=last[2][:, at : at + N_TILE],
+                rhs=moving[a][1][:, at : at + N_TILE].bitcast(E5M2X4),
+                rhs_scale=moving[a][2][:, at : at + N_TILE],
                 start=start,
-                stop=True,
+                stop=stop,
             )
 
-        def keep_partial(copy, m):
-            copy(out=partial[m][:], in_=acc[m, 1][:, HALF:])
-
-        def finish_late(m):
-            nc.vector.tensor_tensor(
-                out=rows[m][:, H - HALF :], in0=acc[m, 0][:, HALF:], in1=partial[m][:], op=mybir.AluOpType.add
+        def store(src, width, h0, m0, count):
+            nc.sync.dma_start(
+                out=out[m0 * M_TILE : (m0 + count) * M_TILE, h0 : h0 + width].rearrange("(i p) h -> p i h", i=count),
+                in_=src[:, m0 * width : (m0 + count) * width].rearrange("p (i h) -> p i h", i=count),
             )
 
-        def drain(copy, m, n, lo=0, hi=N_TILE):
-            copy(out=rows[m][:, n * N_TILE + lo : n * N_TILE + hi], in_=acc[m, n][:, lo:hi])
-
-        def store(m, lo, hi):
-            nc.sync.dma_start(out=out[m * M_TILE : (m + 1) * M_TILE, lo:hi], in_=rows[m][:, lo:hi])
+        def block(tile, m, width=HALF):
+            return tile[:, m * width : (m + 1) * width]
 
         dy0 = load_dy(0, 0, H)
         load_x4_scales()
@@ -170,59 +151,90 @@ def tile_mix_dwsav_none_kernel(tc, x4_words, x4_scales, x8, dy, out):
         load_x4_codes(0, D)
         dy10 = load_dy(1, 0, N_TILE)
         dy20 = load_dy(2, 0, N_TILE)
-        dy11 = load_dy(1, N_TILE, H)
-        dy21a = load_dy(2, N_TILE, H - HALF)
-        dy21b = load_dy(2, H - HALF, H)
+        late = []
+        for g in range(2):
+            for a in (1, 2):
+                late.append((a, g, load_dy(a, N_TILE + g * HALF, N_TILE + (g + 1) * HALF)))
 
-        def in_halves(raw, a, n, v_cols):
-            interleave(vector, raw, 0, moving[a, n], 0, HALF)
-            shared(raw, HALF, moving[a, n], HALF, HALF, v_cols)
-            quantize_dy(a, n, 0, HALF)
-            quantize_dy(a, n, HALF, HALF)
+        def in_halves(raw, a, v_cols):
+            interleave(vector, raw, 0, moving[a], 0, HALF)
+            shared(raw, HALF, moving[a], HALF, HALF, v_cols)
+            quantize_dy(a, 0, HALF)
+            quantize_dy(a, HALF, HALF)
 
+        eng = {"s": scalar, "v": vector}
         for n in range(H_TILES):
-            shared(dy0, n * N_TILE, moving[0, n], 0, N_TILE, 288)
+            shared(dy0, n * N_TILE, moving[0], n * N_TILE, N_TILE, 288)
         for n in range(H_TILES):
-            quantize_dy(0, n)
+            quantize_dy(0, n * N_TILE, N_TILE)
         for a, raw in ((1, x1), (2, x2)):
             shared(raw, 0, stationary[a], 0, D, 288)
             quantize_x8(a)
-        for m in range(M_TILES):
-            multiply(0, m, 0)
-        for m in (0, 1):
-            multiply(0, m, 1)
-        for a, raw in ((1, dy10), (2, dy20)):
-            in_halves(raw, a, 0, 64)
+        if PPOS == 0:
             for m in range(M_TILES):
-                multiply(a, m, 0)
-        for m in (2, 3):
-            multiply(0, m, 1)
+                multiply(0, m, 1, N_TILE, True, True)
+            for m in range(M_TILES):
+                eng[PD](out=block(partial, m), in_=acc[m, 1][:, HALF:])
+        for m in range(M_TILES):
+            multiply(0, m, 0, 0, True, False)
+        if PPOS == 1:
+            for m in range(M_TILES):
+                multiply(0, m, 1, N_TILE, True, True)
+        for m in range(E0):
+            multiply(0, m, 1, HALF, True, False)
+        in_halves(dy10, 1, V20)
+        if PPOS == 1:
+            for m in range(M_TILES):
+                eng[PD](out=block(partial, m), in_=acc[m, 1][:, HALF:])
+        for m in range(M_TILES):
+            multiply(1, m, 0, 0, False, False)
+        for m in range(E0, M_TILES):
+            multiply(0, m, 1, HALF, True, False)
+        in_halves(dy20, 2, V20)
+        for m in range(M_TILES):
+            multiply(2, m, 0, 0, False, True)
+        for m in range(M_TILES):
+            scalar(out=block(left, m, N_TILE), in_=acc[m, 0][:])
+            store(left, N_TILE, 0, m, 1)
 
-        drain(scalar, 0, 0)
-        store(0, 0, N_TILE)
-        in_halves(dy11, 1, 1, 128)
+        def grouped_stores(src, h0, m, sizes):
+            ends = [sum(sizes[: i + 1]) for i in range(len(sizes))]
+            if m + 1 in ends:
+                i = ends.index(m + 1)
+                store(src, HALF, h0, m + 1 - sizes[i], sizes[i])
+
+        pending = []
+        for step, (a, g, raw) in enumerate(late):
+            h0 = N_TILE + g * HALF
+            at = 0
+            for w in QS[step]:
+                shared(raw, at, moving[a], h0 + at, w, max(0, min(w, VS[step] - at)))
+                at = at + w
+                for f in pending:
+                    f()
+                pending = []
+
+            def rest(a=a, g=g, h0=h0, step=step, skip=0):
+                at = 0
+                for i, w in enumerate(QS[step]):
+                    if i >= skip:
+                        quantize_dy(a, h0 + at, w)
+                    at = at + w
+                for m in range(M_TILES):
+                    if g == 0:
+                        multiply(a, m, 1, HALF, False, a == 2)
+                    else:
+                        multiply(a, m, 0, N_TILE, a == 1, a == 2)
+                if (a, g) == (2, 0):
+                    for m in range(M_TILES):
+                        eng[BD[m]](out=block(mid, m), in_=acc[m, 1][:, HALF:])
+                        grouped_stores(mid, N_TILE, m, BM)
+
+            if step < PIPE:
+                quantize_dy(a, h0, QS[step][0])
+                pending = [lambda rest=rest: rest(skip=1)]
+            else:
+                rest()
         for m in range(M_TILES):
-            multiply(1, m, 1)
-        for m in range(1, M_TILES):
-            drain(scalar, m, 0)
-            store(m, 0, N_TILE)
-        interleave(vector, dy21a, 0, last, 0, 128)
-        interleave(vector, dy21a, 128, last, 128, 128)
-        quantize(last, E5M2X4, 0, 128)
-        quantize(last, E5M2X4, 128, 128)
-        for m in range(M_TILES):
-            multiply_last(m, 0, acc[m, 1], False)
-        interleave(vector, dy21b, 0, last, 2 * HALF, 128)
-        shared(dy21b, 128, last, 2 * HALF + 128, 128, 32)
-        quantize(last, E5M2X4, 2 * HALF, 128)
-        quantize(last, E5M2X4, 2 * HALF + 128, 128)
-        for m in range(M_TILES):
-            multiply_last(m, HALF, acc[m, 0], True)
-        for m in range(M_TILES):
-            copy = scalar if m % 2 == 0 else vector
-            drain(copy, m, 1, 0, HALF)
-            store(m, N_TILE, H - HALF)
-            keep_partial(vector if m == 1 else scalar, m)
-        for m in range(M_TILES):
-            finish_late(m)
-            store(m, H - HALF, H)
+            nc.vector.tensor_tensor(out=block(right, m), in0=acc[m, 0][:, HALF:], in1=block(partial, m), op=mybir.AluOpType.add)
+            grouped_stores(right, H - HALF, m, CM)

@@ -23,17 +23,12 @@ FLOPS = 2 * T * D * H
 
 H_TILES = H // N_TILE
 HALF = N_TILE // 2
-V20 = 64
-VS = [256, 256, 256, 256]
-BD = "ssss"
-BM = [2, 2]
-CM = [1, 1, 1, 1]
-PD = "s"
-QS = [[128, 128], [128, 128], [128, 128], [128, 64, 64]]
-E0 = 4
-PPOS = 0
-VA = 0
-PIPE = 0
+WIDE = N_TILE + HALF
+V_EARLY = 288
+V_DY2 = 320
+V_DY1 = 384
+S_X2 = 128
+LATE_CUT = [128, 64, 64]
 
 
 def tile_mix_dwsav_none_kernel(tc, x4_words, x4_scales, x8, dy, out):
@@ -147,94 +142,74 @@ def tile_mix_dwsav_none_kernel(tc, x4_words, x4_scales, x8, dy, out):
         dy0 = load_dy(0, 0, H)
         load_x4_scales()
         x1 = load_x8(1, 0, D)
-        x2 = load_x8(2, 0, D)
         load_x4_codes(0, D)
-        dy10 = load_dy(1, 0, N_TILE)
-        dy20 = load_dy(2, 0, N_TILE)
-        late = []
-        for g in range(2):
-            for a in (1, 2):
-                late.append((a, g, load_dy(a, N_TILE + g * HALF, N_TILE + (g + 1) * HALF)))
+        dy2 = load_dy(2, 0, N_TILE)
+        dy1 = load_dy(1, 0, N_TILE)
+        x2 = load_x8(2, 0, D)
+        dy1_mid = load_dy(1, N_TILE, WIDE)
+        dy2_mid = load_dy(2, N_TILE, WIDE)
+        dy1_last = load_dy(1, WIDE, H)
+        dy2_last = load_dy(2, WIDE, H)
 
         def in_halves(raw, a, v_cols):
             interleave(vector, raw, 0, moving[a], 0, HALF)
-            shared(raw, HALF, moving[a], HALF, HALF, v_cols)
+            shared(raw, HALF, moving[a], HALF, HALF, v_cols - HALF)
             quantize_dy(a, 0, HALF)
             quantize_dy(a, HALF, HALF)
 
-        eng = {"s": scalar, "v": vector}
-        for n in range(H_TILES):
-            shared(dy0, n * N_TILE, moving[0], n * N_TILE, N_TILE, 288)
-        for n in range(H_TILES):
+        for n in (1, 0):
+            shared(dy0, n * N_TILE, moving[0], n * N_TILE, N_TILE, V_EARLY)
+        for n in (1, 0):
             quantize_dy(0, n * N_TILE, N_TILE)
-        for a, raw in ((1, x1), (2, x2)):
-            shared(raw, 0, stationary[a], 0, D, 288)
-            quantize_x8(a)
-        if PPOS == 0:
-            for m in range(M_TILES):
-                multiply(0, m, 1, N_TILE, True, True)
-            for m in range(M_TILES):
-                eng[PD](out=block(partial, m), in_=acc[m, 1][:, HALF:])
+        shared(x1, 0, stationary[1], 0, D, V_EARLY)
+        quantize_x8(1)
+        in_halves(dy2, 2, V_DY2)
+        for m in range(M_TILES):
+            multiply(0, m, 1, N_TILE, True, True)
+        for m in range(M_TILES):
+            scalar(out=block(partial, m), in_=acc[m, 1][:, HALF:])
         for m in range(M_TILES):
             multiply(0, m, 0, 0, True, False)
-        if PPOS == 1:
-            for m in range(M_TILES):
-                multiply(0, m, 1, N_TILE, True, True)
-        for m in range(E0):
+        for m in range(M_TILES):
             multiply(0, m, 1, HALF, True, False)
-        in_halves(dy10, 1, V20)
-        if PPOS == 1:
-            for m in range(M_TILES):
-                eng[PD](out=block(partial, m), in_=acc[m, 1][:, HALF:])
+        in_halves(dy1, 1, V_DY1)
         for m in range(M_TILES):
             multiply(1, m, 0, 0, False, False)
-        for m in range(E0, M_TILES):
-            multiply(0, m, 1, HALF, True, False)
-        in_halves(dy20, 2, V20)
+
+        interleave(scalar, x2, D - S_X2, stationary[2], D - S_X2, S_X2)
+        interleave(vector, x2, 0, stationary[2], 0, M_TILE)
         for m in range(M_TILES):
+            ahead = (m + 1) * M_TILE
+            if ahead < D - S_X2:
+                interleave(vector, x2, ahead, stationary[2], ahead, M_TILE)
+            quantize_x8(2, m * M_TILE, M_TILE)
             multiply(2, m, 0, 0, False, True)
-        for m in range(M_TILES):
             scalar(out=block(left, m, N_TILE), in_=acc[m, 0][:])
             store(left, N_TILE, 0, m, 1)
 
-        def grouped_stores(src, h0, m, sizes):
-            ends = [sum(sizes[: i + 1]) for i in range(len(sizes))]
-            if m + 1 in ends:
-                i = ends.index(m + 1)
-                store(src, HALF, h0, m + 1 - sizes[i], sizes[i])
+        def piece(raw, a, h0):
+            starts = [sum(LATE_CUT[:i]) for i in range(len(LATE_CUT))]
+            for at, w in zip(starts, LATE_CUT):
+                interleave(vector, raw, at, moving[a], h0 + at, w)
+            for at, w in zip(starts, LATE_CUT):
+                quantize_dy(a, h0 + at, w)
 
-        pending = []
-        for step, (a, g, raw) in enumerate(late):
-            h0 = N_TILE + g * HALF
-            at = 0
-            for w in QS[step]:
-                shared(raw, at, moving[a], h0 + at, w, max(0, min(w, VS[step] - at)))
-                at = at + w
-                for f in pending:
-                    f()
-                pending = []
-
-            def rest(a=a, g=g, h0=h0, step=step, skip=0):
-                at = 0
-                for i, w in enumerate(QS[step]):
-                    if i >= skip:
-                        quantize_dy(a, h0 + at, w)
-                    at = at + w
-                for m in range(M_TILES):
-                    if g == 0:
-                        multiply(a, m, 1, HALF, False, a == 2)
-                    else:
-                        multiply(a, m, 0, N_TILE, a == 1, a == 2)
-                if (a, g) == (2, 0):
-                    for m in range(M_TILES):
-                        eng[BD[m]](out=block(mid, m), in_=acc[m, 1][:, HALF:])
-                        grouped_stores(mid, N_TILE, m, BM)
-
-            if step < PIPE:
-                quantize_dy(a, h0, QS[step][0])
-                pending = [lambda rest=rest: rest(skip=1)]
-            else:
-                rest()
+        piece(dy1_mid, 1, N_TILE)
+        for m in range(M_TILES):
+            multiply(1, m, 1, HALF, False, False)
+        piece(dy2_mid, 2, N_TILE)
+        for m in range(M_TILES):
+            multiply(2, m, 1, HALF, False, True)
+        for m in range(M_TILES):
+            scalar(out=block(mid, m), in_=acc[m, 1][:, HALF:])
+            if m % 2 == 1:
+                store(mid, HALF, N_TILE, m - 1, 2)
+        piece(dy1_last, 1, WIDE)
+        for m in range(M_TILES):
+            multiply(1, m, 0, N_TILE, True, False)
+        piece(dy2_last, 2, WIDE)
+        for m in range(M_TILES):
+            multiply(2, m, 0, N_TILE, False, True)
         for m in range(M_TILES):
             nc.vector.tensor_tensor(out=block(right, m), in0=acc[m, 0][:, HALF:], in1=block(partial, m), op=mybir.AluOpType.add)
-            grouped_stores(right, H - HALF, m, CM)
+            store(right, HALF, WIDE, m, 1)

@@ -24,11 +24,12 @@ FLOPS = 2 * T * D * H
 H_TILES = H // N_TILE
 HALF = N_TILE // 2
 WIDE = N_TILE + HALF
+QUARTER = HALF // 2
 V_EARLY = 288
 V_DY2 = 320
 V_DY1 = 384
-S_X2 = 128
-LATE_CUT = [128, 64, 64]
+S_X2 = 192
+LAST_CUT = [128, 64, 64]
 
 
 def tile_mix_dwsav_none_kernel(tc, x4_words, x4_scales, x8, dy, out):
@@ -176,38 +177,45 @@ def tile_mix_dwsav_none_kernel(tc, x4_words, x4_scales, x8, dy, out):
         for m in range(M_TILES):
             multiply(1, m, 0, 0, False, False)
 
-        interleave(scalar, x2, D - S_X2, stationary[2], D - S_X2, S_X2)
-        interleave(vector, x2, 0, stationary[2], 0, M_TILE)
-        for m in range(M_TILES):
-            ahead = (m + 1) * M_TILE
-            if ahead < D - S_X2:
-                interleave(vector, x2, ahead, stationary[2], ahead, M_TILE)
+        def finish_left(m):
             quantize_x8(2, m * M_TILE, M_TILE)
             multiply(2, m, 0, 0, False, True)
             scalar(out=block(left, m, N_TILE), in_=acc[m, 0][:])
-            store(left, N_TILE, 0, m, 1)
+            if m % 2 == 1:
+                store(left, N_TILE, 0, m - 1, 2)
 
-        def piece(raw, a, h0):
-            starts = [sum(LATE_CUT[:i]) for i in range(len(LATE_CUT))]
-            for at, w in zip(starts, LATE_CUT):
+        interleave(scalar, x2, D - S_X2, stationary[2], D - S_X2, S_X2)
+        interleave(vector, x2, 0, stationary[2], 0, M_TILE)
+        interleave(vector, x2, M_TILE, stationary[2], M_TILE, M_TILE)
+        finish_left(0)
+        interleave(vector, x2, 2 * M_TILE, stationary[2], 2 * M_TILE, D - S_X2 - 2 * M_TILE)
+        finish_left(1)
+        for i in range(2):
+            interleave(vector, dy1_mid, i * QUARTER, moving[1], N_TILE + i * QUARTER, QUARTER)
+            finish_left(2 + i)
+        for i in range(2):
+            quantize_dy(1, N_TILE + i * QUARTER, QUARTER)
+
+        def piece(raw, a, h0, widths):
+            starts = [sum(widths[:i]) for i in range(len(widths))]
+            for at, w in zip(starts, widths):
                 interleave(vector, raw, at, moving[a], h0 + at, w)
-            for at, w in zip(starts, LATE_CUT):
+            for at, w in zip(starts, widths):
                 quantize_dy(a, h0 + at, w)
 
-        piece(dy1_mid, 1, N_TILE)
         for m in range(M_TILES):
             multiply(1, m, 1, HALF, False, False)
-        piece(dy2_mid, 2, N_TILE)
+        piece(dy2_mid, 2, N_TILE, [QUARTER, QUARTER])
         for m in range(M_TILES):
             multiply(2, m, 1, HALF, False, True)
         for m in range(M_TILES):
             scalar(out=block(mid, m), in_=acc[m, 1][:, HALF:])
             if m % 2 == 1:
                 store(mid, HALF, N_TILE, m - 1, 2)
-        piece(dy1_last, 1, WIDE)
+        piece(dy1_last, 1, WIDE, [QUARTER, QUARTER])
         for m in range(M_TILES):
             multiply(1, m, 0, N_TILE, True, False)
-        piece(dy2_last, 2, WIDE)
+        piece(dy2_last, 2, WIDE, LAST_CUT)
         for m in range(M_TILES):
             multiply(2, m, 0, N_TILE, False, True)
         for m in range(M_TILES):

@@ -18,18 +18,21 @@ K_PASS = P * PACK
 M_TILE = 128
 N_TILE = 512
 M_TILES = D // M_TILE
-
-FLOPS = 2 * T * D * H
-
-H_TILES = H // N_TILE
 HALF = N_TILE // 2
-WIDE = N_TILE + HALF
 QUARTER = HALF // 2
+WIDE = N_TILE + HALF
+MID_AT = N_TILE + HALF
+LAST_AT = MID_AT + N_TILE
+CODES_W = LAST_AT + HALF
 V_EARLY = 288
 V_DY2 = 320
 V_DY1 = 384
 S_X2 = 192
+LEFT_STORES = {0: 1, 1: 1, 3: 2}
 LAST_CUT = [128, 64, 64]
+OWN = (1, 3)
+
+FLOPS = 2 * T * D * H
 
 
 def tile_mix_dwsav_none_kernel(tc, x4_words, x4_scales, x8, dy, out):
@@ -53,21 +56,8 @@ def tile_mix_dwsav_none_kernel(tc, x4_words, x4_scales, x8, dy, out):
         def load_dy(a, lo, hi):
             return load("dy%d_%d" % (a, lo), dy, a * K_PASS, lo, hi)
 
-        def load_x8(a, lo, hi):
-            return load("x8_%d_%d" % (a, lo), x8, (a - 1) * K_PASS, lo, hi)
-
-        def load_x4_codes(lo, hi):
-            nc.sync.dma_start(
-                out=x4_codes[:, 2 * lo : 2 * hi].bitcast(I32),
-                in_=x4_words[0, :, 2 * lo : 2 * hi].bitcast(I32),
-            )
-
-        def load_x4_scales():
-            for q in range(4):
-                nc.sync.dma_start(
-                    out=x4_plane[32 * q : 32 * q + 4, :].bitcast(I32),
-                    in_=x4_scales[0, 4 * q : 4 * q + 4, :].bitcast(I32),
-                )
+        def load_x8(a):
+            return load("x8_%d" % a, x8, (a - 1) * K_PASS, 0, D)
 
         def operand(name, width):
             grouped = keep.tile([P, PACK * width], BF16, name="grouped_" + name, align_bytes=64)
@@ -75,18 +65,21 @@ def tile_mix_dwsav_none_kernel(tc, x4_words, x4_scales, x8, dy, out):
             plane = keep.tile([P, width], U8, name="plane_" + name, align_bytes=64)
             return grouped, codes, plane
 
-        acc, moving, stationary = {}, {}, {}
         left = keep.tile([M_TILE, M_TILES * N_TILE], F32, name="left", align_bytes=64)
         mid = keep.tile([M_TILE, M_TILES * HALF], F32, name="mid", align_bytes=64)
-        right = keep.tile([M_TILE, M_TILES * HALF], F32, name="right", align_bytes=64)
+        last = keep.tile([M_TILE, M_TILES * HALF], F32, name="last", align_bytes=64)
         partial = keep.tile([M_TILE, M_TILES * HALF], F32, name="partial", align_bytes=64)
-        for m in range(M_TILES):
-            for n in range(H_TILES):
-                acc[m, n] = psum.tile([M_TILE, N_TILE], F32, name="acc_%d%d" % (m, n))
+        left_bank = [psum.tile([M_TILE, N_TILE], F32, name="left_bank%d" % m) for m in range(M_TILES)]
+        pair_bank = [psum.tile([M_TILE, N_TILE], F32, name="pair_bank%d" % i) for i in range(2)]
+        own_bank = {m: psum.tile([M_TILE, N_TILE], F32, name="own_bank%d" % m) for m in OWN}
+        borrowed = [m for m in range(M_TILES) if m not in OWN]
+        last_bank = [own_bank.get(m, left_bank[m]) for m in range(M_TILES)]
+        moving = {a: operand("dy%d" % a, CODES_W) for a in range(3)}
+        stationary = {a: operand("x8_%d" % a, D) for a in (1, 2)}
         for a in range(3):
-            moving[a] = operand("dy%d" % a, H)
-        for a in (1, 2):
-            stationary[a] = operand("x8_%d" % a, D)
+            for at in (MID_AT - HALF, MID_AT + HALF):
+                nc.vector.memset(moving[a][1][:, at : at + HALF], 0)
+                nc.vector.memset(moving[a][2][:, at : at + HALF].bitcast(I32), 0)
 
         def interleave(copy, raw, lo, op, at, width):
             copy(
@@ -95,10 +88,8 @@ def tile_mix_dwsav_none_kernel(tc, x4_words, x4_scales, x8, dy, out):
             )
 
         def shared(raw, lo, op, at, width, v_cols):
-            if v_cols > 0:
-                interleave(vector, raw, lo, op, at, v_cols)
-            if v_cols < width:
-                interleave(scalar, raw, lo + v_cols, op, at + v_cols, width - v_cols)
+            interleave(vector, raw, lo, op, at, v_cols)
+            interleave(scalar, raw, lo + v_cols, op, at + v_cols, width - v_cols)
 
         def quantize(op, fmt, at, width):
             nc.vector.quantize_mx(
@@ -110,9 +101,6 @@ def tile_mix_dwsav_none_kernel(tc, x4_words, x4_scales, x8, dy, out):
         def quantize_dy(a, at, width):
             quantize(moving[a], E5M2X4, at, width)
 
-        def quantize_x8(a, at=0, width=D):
-            quantize(stationary[a], E4M3X4, at, width)
-
         def multiply(a, m, bank, at, start, stop):
             cols = slice(m * M_TILE, (m + 1) * M_TILE)
             if a == 0:
@@ -122,7 +110,7 @@ def tile_mix_dwsav_none_kernel(tc, x4_words, x4_scales, x8, dy, out):
                 lhsT = stationary[a][1][:, cols].bitcast(E4M3X4)
                 lhsT_scale = stationary[a][2][:, cols]
             nc.tensor.matmul_mx(
-                out=acc[m, bank][:],
+                out=bank[:],
                 lhsT=lhsT,
                 lhsT_scale=lhsT_scale,
                 rhs=moving[a][1][:, at : at + N_TILE].bitcast(E5M2X4),
@@ -130,6 +118,9 @@ def tile_mix_dwsav_none_kernel(tc, x4_words, x4_scales, x8, dy, out):
                 start=start,
                 stop=stop,
             )
+
+        def multiply_mid(a, m):
+            multiply(a, m, pair_bank[m // 2], MID_AT - (m % 2) * HALF, a == 0 and m % 2 == 0, a == 2 and m % 2 == 1)
 
         def store(src, width, h0, m0, count):
             nc.sync.dma_start(
@@ -141,12 +132,16 @@ def tile_mix_dwsav_none_kernel(tc, x4_words, x4_scales, x8, dy, out):
             return tile[:, m * width : (m + 1) * width]
 
         dy0 = load_dy(0, 0, H)
-        load_x4_scales()
-        x1 = load_x8(1, 0, D)
-        load_x4_codes(0, D)
+        for q in range(4):
+            nc.sync.dma_start(
+                out=x4_plane[32 * q : 32 * q + 4, :].bitcast(I32),
+                in_=x4_scales[0, 4 * q : 4 * q + 4, :].bitcast(I32),
+            )
+        x1 = load_x8(1)
+        nc.sync.dma_start(out=x4_codes[:].bitcast(I32), in_=x4_words[0].bitcast(I32))
         dy2 = load_dy(2, 0, N_TILE)
         dy1 = load_dy(1, 0, N_TILE)
-        x2 = load_x8(2, 0, D)
+        x2 = load_x8(2)
         dy1_mid = load_dy(1, N_TILE, WIDE)
         dy2_mid = load_dy(2, N_TILE, WIDE)
         dy1_last = load_dy(1, WIDE, H)
@@ -158,31 +153,42 @@ def tile_mix_dwsav_none_kernel(tc, x4_words, x4_scales, x8, dy, out):
             quantize_dy(a, 0, HALF)
             quantize_dy(a, HALF, HALF)
 
-        for n in (1, 0):
-            shared(dy0, n * N_TILE, moving[0], n * N_TILE, N_TILE, V_EARLY)
-        for n in (1, 0):
-            quantize_dy(0, n * N_TILE, N_TILE)
+        def piece(raw, a, at0, widths):
+            starts = [sum(widths[:i]) for i in range(len(widths))]
+            for at, w in zip(starts, widths):
+                interleave(vector, raw, at, moving[a], at0 + at, w)
+            for at, w in zip(starts, widths):
+                quantize_dy(a, at0 + at, w)
+
+        shared(dy0, 0, moving[0], 0, N_TILE, V_EARLY)
+        interleave(vector, dy0, N_TILE, moving[0], MID_AT, HALF)
+        interleave(scalar, dy0, WIDE, moving[0], LAST_AT, HALF)
+        quantize_dy(0, 0, N_TILE)
+        quantize_dy(0, MID_AT, HALF)
+        quantize_dy(0, LAST_AT, HALF)
         shared(x1, 0, stationary[1], 0, D, V_EARLY)
-        quantize_x8(1)
+        quantize(stationary[1], E4M3X4, 0, D)
         in_halves(dy2, 2, V_DY2)
+        for i, m in enumerate(borrowed):
+            multiply(0, m, pair_bank[i], LAST_AT - HALF, True, True)
+        for i, m in enumerate(borrowed):
+            scalar(out=block(partial, m), in_=pair_bank[i][:, HALF:])
         for m in range(M_TILES):
-            multiply(0, m, 1, N_TILE, True, True)
+            multiply(0, m, left_bank[m], 0, True, False)
+        for m in OWN:
+            multiply(0, m, own_bank[m], LAST_AT - HALF, True, False)
         for m in range(M_TILES):
-            scalar(out=block(partial, m), in_=acc[m, 1][:, HALF:])
-        for m in range(M_TILES):
-            multiply(0, m, 0, 0, True, False)
-        for m in range(M_TILES):
-            multiply(0, m, 1, HALF, True, False)
+            multiply_mid(0, m)
         in_halves(dy1, 1, V_DY1)
         for m in range(M_TILES):
-            multiply(1, m, 0, 0, False, False)
+            multiply(1, m, left_bank[m], 0, False, False)
 
         def finish_left(m):
-            quantize_x8(2, m * M_TILE, M_TILE)
-            multiply(2, m, 0, 0, False, True)
-            scalar(out=block(left, m, N_TILE), in_=acc[m, 0][:])
-            if m % 2 == 1:
-                store(left, N_TILE, 0, m - 1, 2)
+            quantize(stationary[2], E4M3X4, m * M_TILE, M_TILE)
+            multiply(2, m, left_bank[m], 0, False, True)
+            scalar(out=block(left, m, N_TILE), in_=left_bank[m][:])
+            if m in LEFT_STORES:
+                store(left, N_TILE, 0, m + 1 - LEFT_STORES[m], LEFT_STORES[m])
 
         interleave(scalar, x2, D - S_X2, stationary[2], D - S_X2, S_X2)
         interleave(vector, x2, 0, stationary[2], 0, M_TILE)
@@ -191,33 +197,27 @@ def tile_mix_dwsav_none_kernel(tc, x4_words, x4_scales, x8, dy, out):
         interleave(vector, x2, 2 * M_TILE, stationary[2], 2 * M_TILE, D - S_X2 - 2 * M_TILE)
         finish_left(1)
         for i in range(2):
-            interleave(vector, dy1_mid, i * QUARTER, moving[1], N_TILE + i * QUARTER, QUARTER)
+            interleave(vector, dy1_mid, i * QUARTER, moving[1], MID_AT + i * QUARTER, QUARTER)
             finish_left(2 + i)
         for i in range(2):
-            quantize_dy(1, N_TILE + i * QUARTER, QUARTER)
-
-        def piece(raw, a, h0, widths):
-            starts = [sum(widths[:i]) for i in range(len(widths))]
-            for at, w in zip(starts, widths):
-                interleave(vector, raw, at, moving[a], h0 + at, w)
-            for at, w in zip(starts, widths):
-                quantize_dy(a, h0 + at, w)
-
+            quantize_dy(1, MID_AT + i * QUARTER, QUARTER)
         for m in range(M_TILES):
-            multiply(1, m, 1, HALF, False, False)
-        piece(dy2_mid, 2, N_TILE, [QUARTER, QUARTER])
+            multiply_mid(1, m)
+        piece(dy2_mid, 2, MID_AT, [QUARTER, QUARTER])
         for m in range(M_TILES):
-            multiply(2, m, 1, HALF, False, True)
+            multiply_mid(2, m)
+        for i in range(2):
+            scalar(out=block(mid, i, N_TILE), in_=pair_bank[i][:])
+            store(mid, HALF, N_TILE, 2 * i, 2)
+        piece(dy1_last, 1, LAST_AT, [QUARTER, QUARTER])
         for m in range(M_TILES):
-            scalar(out=block(mid, m), in_=acc[m, 1][:, HALF:])
-            if m % 2 == 1:
-                store(mid, HALF, N_TILE, m - 1, 2)
-        piece(dy1_last, 1, WIDE, [QUARTER, QUARTER])
+            multiply(1, m, last_bank[m], LAST_AT - HALF, m in borrowed, False)
+        piece(dy2_last, 2, LAST_AT, LAST_CUT)
         for m in range(M_TILES):
-            multiply(1, m, 0, N_TILE, True, False)
-        piece(dy2_last, 2, WIDE, LAST_CUT)
+            multiply(2, m, last_bank[m], LAST_AT - HALF, False, True)
         for m in range(M_TILES):
-            multiply(2, m, 0, N_TILE, False, True)
-        for m in range(M_TILES):
-            nc.vector.tensor_tensor(out=block(right, m), in0=acc[m, 0][:, HALF:], in1=block(partial, m), op=mybir.AluOpType.add)
-            store(right, HALF, WIDE, m, 1)
+            if m in OWN:
+                scalar(out=block(last, m), in_=last_bank[m][:, HALF:])
+            else:
+                nc.vector.tensor_tensor(out=block(last, m), in0=last_bank[m][:, HALF:], in1=block(partial, m), op=mybir.AluOpType.add)
+            store(last, HALF, WIDE, m, 1)

@@ -20,17 +20,24 @@ N_TILE = 512
 M_TILES = D // M_TILE
 HALF = N_TILE // 2
 QUARTER = HALF // 2
-WIDE = N_TILE + HALF
+MID_H = N_TILE
+LAST_H = N_TILE + HALF
 MID_AT = N_TILE + HALF
 LAST_AT = MID_AT + N_TILE
-CODES_W = LAST_AT + HALF
+LAST_WINDOW = LAST_AT - HALF
+DY_WORDS = LAST_AT + HALF
+RUN = 4
+
+OWN_BANK = (1, 3)
+
+ALIGN = 256
+
 V_EARLY = 288
 V_DY2 = 320
 V_DY1 = 384
 S_X2 = 192
-LEFT_STORES = {0: 1, 1: 1, 3: 2}
-LAST_CUT = [128, 64, 64]
-OWN = (1, 3)
+LATE_PARTS = (QUARTER, QUARTER)
+LAST_PARTS = (QUARTER, QUARTER // 2, QUARTER // 2)
 
 FLOPS = 2 * T * D * H
 
@@ -43,12 +50,12 @@ def tile_mix_dwsav_none_kernel(tc, x4_words, x4_scales, x8, dy, out):
         ctx.enter_context(tc.manual_schedule())
         vector, scalar = nc.vector.tensor_copy, nc.scalar.copy
 
-        x4_codes = keep.tile([P, 2 * D], U8, name="x4_codes", align_bytes=64)
-        x4_plane = keep.tile([P, D], U8, name="x4_plane", align_bytes=64)
+        x4_codes = keep.tile([P, 2 * D], U8, name="x4_codes", align_bytes=ALIGN)
+        x4_plane = keep.tile([P, D], U8, name="x4_plane", align_bytes=ALIGN)
         nc.vector.memset(x4_plane[:].bitcast(I32), 0)
 
         def load(name, src, row0, lo, hi):
-            raw = keep.tile([P, PACK, hi - lo], F32, name="raw_" + name, align_bytes=64)
+            raw = keep.tile([P, PACK, hi - lo], F32, name="raw_" + name, align_bytes=ALIGN)
             rows = src[row0 : row0 + K_PASS, lo:hi]
             nc.sync.dma_start(out=raw[:], in_=rows.rearrange("(p j) w -> p j w", j=PACK))
             return raw
@@ -60,21 +67,21 @@ def tile_mix_dwsav_none_kernel(tc, x4_words, x4_scales, x8, dy, out):
             return load("x8_%d" % a, x8, (a - 1) * K_PASS, 0, D)
 
         def operand(name, width):
-            grouped = keep.tile([P, PACK * width], BF16, name="grouped_" + name, align_bytes=64)
-            codes = keep.tile([P, width], U32, name="codes_" + name, align_bytes=64)
-            plane = keep.tile([P, width], U8, name="plane_" + name, align_bytes=64)
+            grouped = keep.tile([P, PACK * width], BF16, name="grouped_" + name, align_bytes=ALIGN)
+            codes = keep.tile([P, width], U32, name="codes_" + name, align_bytes=ALIGN)
+            plane = keep.tile([P, width], U8, name="plane_" + name, align_bytes=ALIGN)
             return grouped, codes, plane
 
-        left = keep.tile([M_TILE, M_TILES * N_TILE], F32, name="left", align_bytes=64)
-        mid = keep.tile([M_TILE, M_TILES * HALF], F32, name="mid", align_bytes=64)
-        last = keep.tile([M_TILE, M_TILES * HALF], F32, name="last", align_bytes=64)
-        partial = keep.tile([M_TILE, M_TILES * HALF], F32, name="partial", align_bytes=64)
+        left = keep.tile([M_TILE, M_TILES * N_TILE], F32, name="left", align_bytes=ALIGN)
+        mid = keep.tile([M_TILE, M_TILES * HALF], F32, name="mid", align_bytes=ALIGN)
+        last = keep.tile([M_TILE, M_TILES * HALF], F32, name="last", align_bytes=ALIGN)
+        partial = keep.tile([M_TILE, M_TILES * HALF], F32, name="partial", align_bytes=ALIGN)
         left_bank = [psum.tile([M_TILE, N_TILE], F32, name="left_bank%d" % m) for m in range(M_TILES)]
-        pair_bank = [psum.tile([M_TILE, N_TILE], F32, name="pair_bank%d" % i) for i in range(2)]
-        own_bank = {m: psum.tile([M_TILE, N_TILE], F32, name="own_bank%d" % m) for m in OWN}
-        borrowed = [m for m in range(M_TILES) if m not in OWN]
+        mid_bank = [psum.tile([M_TILE, N_TILE], F32, name="mid_bank%d" % i) for i in range(M_TILES // 2)]
+        own_bank = {m: psum.tile([M_TILE, N_TILE], F32, name="own_bank%d" % m) for m in OWN_BANK}
+        borrowers = [m for m in range(M_TILES) if m not in OWN_BANK]
         last_bank = [own_bank.get(m, left_bank[m]) for m in range(M_TILES)]
-        moving = {a: operand("dy%d" % a, CODES_W) for a in range(3)}
+        moving = {a: operand("dy%d" % a, DY_WORDS) for a in range(3)}
         stationary = {a: operand("x8_%d" % a, D) for a in (1, 2)}
         for a in range(3):
             for at in (MID_AT - HALF, MID_AT + HALF):
@@ -83,13 +90,13 @@ def tile_mix_dwsav_none_kernel(tc, x4_words, x4_scales, x8, dy, out):
 
         def interleave(copy, raw, lo, op, at, width):
             copy(
-                out=op[0][:, PACK * at : PACK * (at + width)].rearrange("p (c i j) -> p c j i", i=4, j=PACK),
-                in_=raw[:, :, lo : lo + width].rearrange("p j (c i) -> p c j i", i=4),
+                out=op[0][:, PACK * at : PACK * (at + width)].rearrange("p (c i j) -> p c j i", i=RUN, j=PACK),
+                in_=raw[:, :, lo : lo + width].rearrange("p j (c i) -> p c j i", i=RUN),
             )
 
-        def shared(raw, lo, op, at, width, v_cols):
-            interleave(vector, raw, lo, op, at, v_cols)
-            interleave(scalar, raw, lo + v_cols, op, at + v_cols, width - v_cols)
+        def interleave_shared(raw, lo, op, width, v_cols):
+            interleave(vector, raw, lo, op, lo, v_cols)
+            interleave(scalar, raw, lo + v_cols, op, lo + v_cols, width - v_cols)
 
         def quantize(op, fmt, at, width):
             nc.vector.quantize_mx(
@@ -119,8 +126,10 @@ def tile_mix_dwsav_none_kernel(tc, x4_words, x4_scales, x8, dy, out):
                 stop=stop,
             )
 
-        def multiply_mid(a, m):
-            multiply(a, m, pair_bank[m // 2], MID_AT - (m % 2) * HALF, a == 0 and m % 2 == 0, a == 2 and m % 2 == 1)
+        def multiply_mid(a):
+            for m in range(M_TILES):
+                odd = m % 2
+                multiply(a, m, mid_bank[m // 2], MID_AT - odd * HALF, a == 0 and odd == 0, a == 2 and odd == 1)
 
         def store(src, width, h0, m0, count):
             nc.sync.dma_start(
@@ -128,7 +137,7 @@ def tile_mix_dwsav_none_kernel(tc, x4_words, x4_scales, x8, dy, out):
                 in_=src[:, m0 * width : (m0 + count) * width].rearrange("p (i h) -> p i h", i=count),
             )
 
-        def block(tile, m, width=HALF):
+        def block(tile, m, width):
             return tile[:, m * width : (m + 1) * width]
 
         dy0 = load_dy(0, 0, H)
@@ -139,47 +148,48 @@ def tile_mix_dwsav_none_kernel(tc, x4_words, x4_scales, x8, dy, out):
             )
         x1 = load_x8(1)
         nc.sync.dma_start(out=x4_codes[:].bitcast(I32), in_=x4_words[0].bitcast(I32))
-        dy2 = load_dy(2, 0, N_TILE)
-        dy1 = load_dy(1, 0, N_TILE)
+        dy2_left = load_dy(2, 0, N_TILE)
+        dy1_left = load_dy(1, 0, N_TILE)
         x2 = load_x8(2)
-        dy1_mid = load_dy(1, N_TILE, WIDE)
-        dy2_mid = load_dy(2, N_TILE, WIDE)
-        dy1_last = load_dy(1, WIDE, H)
-        dy2_last = load_dy(2, WIDE, H)
+        dy1_mid = load_dy(1, MID_H, LAST_H)
+        dy2_mid = load_dy(2, MID_H, LAST_H)
+        dy1_last = load_dy(1, LAST_H, H)
+        dy2_last = load_dy(2, LAST_H, H)
 
-        def in_halves(raw, a, v_cols):
+        def prepare_left(raw, a, v_cols):
             interleave(vector, raw, 0, moving[a], 0, HALF)
-            shared(raw, HALF, moving[a], HALF, HALF, v_cols - HALF)
+            interleave_shared(raw, HALF, moving[a], HALF, v_cols - HALF)
             quantize_dy(a, 0, HALF)
             quantize_dy(a, HALF, HALF)
 
-        def piece(raw, a, at0, widths):
-            starts = [sum(widths[:i]) for i in range(len(widths))]
-            for at, w in zip(starts, widths):
-                interleave(vector, raw, at, moving[a], at0 + at, w)
-            for at, w in zip(starts, widths):
-                quantize_dy(a, at0 + at, w)
+        def prepare_late(raw, a, at0, parts):
+            starts = [sum(parts[:i]) for i in range(len(parts))]
+            for at, width in zip(starts, parts):
+                interleave(vector, raw, at, moving[a], at0 + at, width)
+            for at, width in zip(starts, parts):
+                quantize_dy(a, at0 + at, width)
 
-        shared(dy0, 0, moving[0], 0, N_TILE, V_EARLY)
-        interleave(vector, dy0, N_TILE, moving[0], MID_AT, HALF)
-        interleave(scalar, dy0, WIDE, moving[0], LAST_AT, HALF)
+        interleave_shared(dy0, 0, moving[0], N_TILE, V_EARLY)
+        interleave(vector, dy0, MID_H, moving[0], MID_AT, HALF)
+        interleave(scalar, dy0, LAST_H, moving[0], LAST_AT, HALF)
         quantize_dy(0, 0, N_TILE)
         quantize_dy(0, MID_AT, HALF)
         quantize_dy(0, LAST_AT, HALF)
-        shared(x1, 0, stationary[1], 0, D, V_EARLY)
+        interleave_shared(x1, 0, stationary[1], D, V_EARLY)
         quantize(stationary[1], E4M3X4, 0, D)
-        in_halves(dy2, 2, V_DY2)
-        for i, m in enumerate(borrowed):
-            multiply(0, m, pair_bank[i], LAST_AT - HALF, True, True)
-        for i, m in enumerate(borrowed):
-            scalar(out=block(partial, m), in_=pair_bank[i][:, HALF:])
+        prepare_left(dy2_left, 2, V_DY2)
+
+        for i, m in enumerate(borrowers):
+            multiply(0, m, mid_bank[i], LAST_WINDOW, True, True)
+        for i, m in enumerate(borrowers):
+            scalar(out=block(partial, m, HALF), in_=mid_bank[i][:, HALF:])
         for m in range(M_TILES):
             multiply(0, m, left_bank[m], 0, True, False)
-        for m in OWN:
-            multiply(0, m, own_bank[m], LAST_AT - HALF, True, False)
-        for m in range(M_TILES):
-            multiply_mid(0, m)
-        in_halves(dy1, 1, V_DY1)
+        for m in OWN_BANK:
+            multiply(0, m, own_bank[m], LAST_WINDOW, True, False)
+        multiply_mid(0)
+
+        prepare_left(dy1_left, 1, V_DY1)
         for m in range(M_TILES):
             multiply(1, m, left_bank[m], 0, False, False)
 
@@ -187,37 +197,43 @@ def tile_mix_dwsav_none_kernel(tc, x4_words, x4_scales, x8, dy, out):
             quantize(stationary[2], E4M3X4, m * M_TILE, M_TILE)
             multiply(2, m, left_bank[m], 0, False, True)
             scalar(out=block(left, m, N_TILE), in_=left_bank[m][:])
-            if m in LEFT_STORES:
-                store(left, N_TILE, 0, m + 1 - LEFT_STORES[m], LEFT_STORES[m])
 
         interleave(scalar, x2, D - S_X2, stationary[2], D - S_X2, S_X2)
         interleave(vector, x2, 0, stationary[2], 0, M_TILE)
         interleave(vector, x2, M_TILE, stationary[2], M_TILE, M_TILE)
         finish_left(0)
+        store(left, N_TILE, 0, 0, 1)
         interleave(vector, x2, 2 * M_TILE, stationary[2], 2 * M_TILE, D - S_X2 - 2 * M_TILE)
         finish_left(1)
+        store(left, N_TILE, 0, 1, 1)
         for i in range(2):
             interleave(vector, dy1_mid, i * QUARTER, moving[1], MID_AT + i * QUARTER, QUARTER)
             finish_left(2 + i)
+        store(left, N_TILE, 0, 2, 2)
+
         for i in range(2):
             quantize_dy(1, MID_AT + i * QUARTER, QUARTER)
+        multiply_mid(1)
+        prepare_late(dy2_mid, 2, MID_AT, LATE_PARTS)
+        multiply_mid(2)
+        for i in range(M_TILES // 2):
+            scalar(out=block(mid, i, N_TILE), in_=mid_bank[i][:])
+            store(mid, HALF, MID_H, 2 * i, 2)
+
+        prepare_late(dy1_last, 1, LAST_AT, LATE_PARTS)
         for m in range(M_TILES):
-            multiply_mid(1, m)
-        piece(dy2_mid, 2, MID_AT, [QUARTER, QUARTER])
+            multiply(1, m, last_bank[m], LAST_WINDOW, m in borrowers, False)
+        prepare_late(dy2_last, 2, LAST_AT, LAST_PARTS)
         for m in range(M_TILES):
-            multiply_mid(2, m)
-        for i in range(2):
-            scalar(out=block(mid, i, N_TILE), in_=pair_bank[i][:])
-            store(mid, HALF, N_TILE, 2 * i, 2)
-        piece(dy1_last, 1, LAST_AT, [QUARTER, QUARTER])
+            multiply(2, m, last_bank[m], LAST_WINDOW, False, True)
         for m in range(M_TILES):
-            multiply(1, m, last_bank[m], LAST_AT - HALF, m in borrowed, False)
-        piece(dy2_last, 2, LAST_AT, LAST_CUT)
-        for m in range(M_TILES):
-            multiply(2, m, last_bank[m], LAST_AT - HALF, False, True)
-        for m in range(M_TILES):
-            if m in OWN:
-                scalar(out=block(last, m), in_=last_bank[m][:, HALF:])
+            if m in OWN_BANK:
+                scalar(out=block(last, m, HALF), in_=last_bank[m][:, HALF:])
             else:
-                nc.vector.tensor_tensor(out=block(last, m), in0=last_bank[m][:, HALF:], in1=block(partial, m), op=mybir.AluOpType.add)
-            store(last, HALF, WIDE, m, 1)
+                nc.vector.tensor_tensor(
+                    out=block(last, m, HALF),
+                    in0=last_bank[m][:, HALF:],
+                    in1=block(partial, m, HALF),
+                    op=mybir.AluOpType.add,
+                )
+            store(last, HALF, LAST_H, m, 1)

@@ -37,7 +37,7 @@ V_DY2 = 320
 V_DY1 = 384
 S_X2 = 192
 LATE_PARTS = (QUARTER, QUARTER)
-LAST_PARTS = (QUARTER, QUARTER // 2, QUARTER // 2)
+LAST_PARTS = (QUARTER // 2, QUARTER // 2)
 
 FLOPS = 2 * T * D * H
 
@@ -154,7 +154,7 @@ def tile_mix_dwsav_none_kernel(tc, x4_words, x4_scales, x8, dy, out):
         dy1_mid = load_dy(1, MID_H, LAST_H)
         dy2_mid = load_dy(2, MID_H, LAST_H)
         dy1_last = load_dy(1, LAST_H, H)
-        dy2_last = load_dy(2, LAST_H, H)
+        dy2_last = [load_dy(2, LAST_H + i * QUARTER, LAST_H + (i + 1) * QUARTER) for i in range(2)]
 
         def prepare_left(raw, a, v_cols):
             interleave(vector, raw, 0, moving[a], 0, HALF)
@@ -223,7 +223,8 @@ def tile_mix_dwsav_none_kernel(tc, x4_words, x4_scales, x8, dy, out):
         prepare_late(dy1_last, 1, LAST_AT, LATE_PARTS)
         for m in range(M_TILES):
             multiply(1, m, last_bank[m], LAST_WINDOW, m in borrowers, False)
-        prepare_late(dy2_last, 2, LAST_AT, LAST_PARTS)
+        for i in range(2):
+            prepare_late(dy2_last[i], 2, LAST_AT + i * QUARTER, LAST_PARTS)
         for m in range(M_TILES):
             multiply(2, m, last_bank[m], LAST_WINDOW, False, True)
         for m in range(M_TILES):

@@ -202,10 +202,9 @@ def tile_mix_dwsav_none_kernel(tc, x4_words, x4_scales, x8, dy, out):
         interleave(vector, x2, 0, stationary[2], 0, M_TILE)
         interleave(vector, x2, M_TILE, stationary[2], M_TILE, M_TILE)
         finish_left(0)
-        store(left, N_TILE, 0, 0, 1)
         interleave(vector, x2, 2 * M_TILE, stationary[2], 2 * M_TILE, D - S_X2 - 2 * M_TILE)
         finish_left(1)
-        store(left, N_TILE, 0, 1, 1)
+        store(left, N_TILE, 0, 0, 2)
         for i in range(2):
             interleave(vector, dy1_mid, i * QUARTER, moving[1], MID_AT + i * QUARTER, QUARTER)
             finish_left(2 + i)
@@ -218,7 +217,7 @@ def tile_mix_dwsav_none_kernel(tc, x4_words, x4_scales, x8, dy, out):
         multiply_mid(2)
         for i in range(M_TILES // 2):
             scalar(out=block(mid, i, N_TILE), in_=mid_bank[i][:])
-            store(mid, HALF, MID_H, 2 * i, 2)
+        store(mid, HALF, MID_H, 0, M_TILES)
 
         prepare_late(dy1_last, 1, LAST_AT, LATE_PARTS)
         for m in range(M_TILES):

@@ -35,9 +35,7 @@ ALIGN = 256
 V_EARLY = 288
 V_DY2 = 320
 V_DY1 = 384
-S_X2 = 192
 LATE_PARTS = (QUARTER, QUARTER)
-LAST_PARTS = (QUARTER // 2, QUARTER // 2)
 
 FLOPS = 2 * T * D * H
 
@@ -198,16 +196,17 @@ def tile_mix_dwsav_none_kernel(tc, x4_words, x4_scales, x8, dy, out):
             multiply(2, m, left_bank[m], 0, False, True)
             scalar(out=block(left, m, N_TILE), in_=left_bank[m][:])
 
-        interleave(scalar, x2, D - S_X2, stationary[2], D - S_X2, S_X2)
-        interleave(vector, x2, 0, stationary[2], 0, M_TILE)
-        interleave(vector, x2, M_TILE, stationary[2], M_TILE, M_TILE)
+        for m in (2, 3):
+            interleave(scalar, x2, m * M_TILE, stationary[2], m * M_TILE, M_TILE)
+        interleave(scalar, dy1_mid, QUARTER, moving[1], MID_AT + QUARTER, QUARTER)
+        for m in (0, 1):
+            interleave(vector, x2, m * M_TILE, stationary[2], m * M_TILE, M_TILE)
         finish_left(0)
-        interleave(vector, x2, 2 * M_TILE, stationary[2], 2 * M_TILE, D - S_X2 - 2 * M_TILE)
         finish_left(1)
         store(left, N_TILE, 0, 0, 2)
-        for i in range(2):
-            interleave(vector, dy1_mid, i * QUARTER, moving[1], MID_AT + i * QUARTER, QUARTER)
-            finish_left(2 + i)
+        finish_left(2)
+        interleave(vector, dy1_mid, 0, moving[1], MID_AT, QUARTER)
+        finish_left(3)
         store(left, N_TILE, 0, 2, 2)
 
         for i in range(2):
@@ -223,7 +222,9 @@ def tile_mix_dwsav_none_kernel(tc, x4_words, x4_scales, x8, dy, out):
         for m in range(M_TILES):
             multiply(1, m, last_bank[m], LAST_WINDOW, m in borrowers, False)
         for i in range(2):
-            prepare_late(dy2_last[i], 2, LAST_AT + i * QUARTER, LAST_PARTS)
+            interleave(vector, dy2_last[i], 0, moving[2], LAST_AT + i * QUARTER, QUARTER)
+        for i in range(2):
+            quantize_dy(2, LAST_AT + i * QUARTER, QUARTER)
         for m in range(M_TILES):
             multiply(2, m, last_bank[m], LAST_WINDOW, False, True)
         for m in range(M_TILES):

@@ -64,11 +64,11 @@ def tile_mix_dwsav_none_kernel(tc, x4_words, x4_scales, x8, dy, out):
         def load_x8(a):
             return load("x8_%d" % a, x8, (a - 1) * K_PASS, 0, D)
 
-        def operand(name, width):
+        def operand(name, width, codes_at, plane_at):
             grouped = keep.tile([P, PACK * width], BF16, name="grouped_" + name, align_bytes=ALIGN)
-            codes = keep.tile([P, width], U32, name="codes_" + name, align_bytes=ALIGN)
-            plane = keep.tile([P, width], U8, name="plane_" + name, align_bytes=ALIGN)
-            return grouped, codes, plane
+            codes = keep.tile([P, width + ALIGN // 4], U32, name="codes_" + name, align_bytes=ALIGN)
+            plane = keep.tile([P, width + ALIGN], U8, name="plane_" + name, align_bytes=ALIGN)
+            return grouped, codes[:, codes_at // 4 : codes_at // 4 + width], plane[:, plane_at : plane_at + width]
 
         left = keep.tile([M_TILE, M_TILES * N_TILE], F32, name="left", align_bytes=ALIGN)
         mid = keep.tile([M_TILE, M_TILES * HALF], F32, name="mid", align_bytes=ALIGN)
@@ -79,8 +79,8 @@ def tile_mix_dwsav_none_kernel(tc, x4_words, x4_scales, x8, dy, out):
         own_bank = {m: psum.tile([M_TILE, N_TILE], F32, name="own_bank%d" % m) for m in OWN_BANK}
         borrowers = [m for m in range(M_TILES) if m not in OWN_BANK]
         last_bank = [own_bank.get(m, left_bank[m]) for m in range(M_TILES)]
-        moving = {a: operand("dy%d" % a, DY_WORDS) for a in range(3)}
-        stationary = {a: operand("x8_%d" % a, D) for a in (1, 2)}
+        moving = {a: operand("dy%d" % a, DY_WORDS, 0, 128) for a in range(3)}
+        stationary = {a: operand("x8_%d" % a, D, 64, 192) for a in (1, 2)}
         for a in range(3):
             for at in (MID_AT - HALF, MID_AT + HALF):
                 nc.vector.memset(moving[a][1][:, at : at + HALF], 0)

@@ -139,10 +139,11 @@ def tile_mix_dwsav_none_kernel(tc, x4_words, x4_scales, x8, dy, out):
             return tile[:, m * width : (m + 1) * width]
 
         dy0 = load_dy(0, 0, H)
-        for q in range(4):
+        for row, count in ((0, 2), (2, 2), (4, 4), (8, 4), (12, 4)):
+            at = 32 * (row // 4) + row % 4
             nc.sync.dma_start(
-                out=x4_plane[32 * q : 32 * q + 4, :].bitcast(I32),
-                in_=x4_scales[0, 4 * q : 4 * q + 4, :].bitcast(I32),
+                out=x4_plane[at : at + count, :].bitcast(I32),
+                in_=x4_scales[0, row : row + count, :].bitcast(I32),
             )
         x1 = load_x8(1)
         nc.sync.dma_start(out=x4_codes[:].bitcast(I32), in_=x4_words[0].bitcast(I32))

@@ -22,10 +22,9 @@ HALF = N_TILE // 2
 QUARTER = HALF // 2
 MID_H = N_TILE
 LAST_H = N_TILE + HALF
-MID_AT = N_TILE + HALF
-LAST_AT = MID_AT + N_TILE
-LAST_WINDOW = LAST_AT - HALF
-DY_WORDS = LAST_AT + HALF
+MID_AT = MID_H
+LAST_AT = LAST_H
+DY_WORDS = H
 RUN = 4
 
 OWN_BANK = (1, 3)
@@ -73,7 +72,6 @@ def tile_mix_dwsav_none_kernel(tc, x4_words, x4_scales, x8, dy, out):
         left = keep.tile([M_TILE, M_TILES * N_TILE], F32, name="left", align_bytes=ALIGN)
         mid = keep.tile([M_TILE, M_TILES * HALF], F32, name="mid", align_bytes=ALIGN)
         last = keep.tile([M_TILE, M_TILES * HALF], F32, name="last", align_bytes=ALIGN)
-        partial = keep.tile([M_TILE, M_TILES * HALF], F32, name="partial", align_bytes=ALIGN)
         left_bank = [psum.tile([M_TILE, N_TILE], F32, name="left_bank%d" % m) for m in range(M_TILES)]
         mid_bank = [psum.tile([M_TILE, N_TILE], F32, name="mid_bank%d" % i) for i in range(M_TILES // 2)]
         own_bank = {m: psum.tile([M_TILE, N_TILE], F32, name="own_bank%d" % m) for m in OWN_BANK}
@@ -81,10 +79,6 @@ def tile_mix_dwsav_none_kernel(tc, x4_words, x4_scales, x8, dy, out):
         last_bank = [own_bank.get(m, left_bank[m]) for m in range(M_TILES)]
         moving = {a: operand("dy%d" % a, DY_WORDS, 0, 128) for a in range(3)}
         stationary = {a: operand("x8_%d" % a, D, 64, 192) for a in (1, 2)}
-        for a in range(3):
-            for at in (MID_AT - HALF, MID_AT + HALF):
-                nc.vector.memset(moving[a][1][:, at : at + HALF], 0)
-                nc.vector.memset(moving[a][2][:, at : at + HALF].bitcast(I32), 0)
 
         def interleave(copy, raw, lo, op, at, width):
             copy(
@@ -106,7 +100,7 @@ def tile_mix_dwsav_none_kernel(tc, x4_words, x4_scales, x8, dy, out):
         def quantize_dy(a, at, width):
             quantize(moving[a], E5M2X4, at, width)
 
-        def multiply(a, m, bank, at, start, stop):
+        def multiply(a, m, bank, at, start, stop, width=N_TILE):
             cols = slice(m * M_TILE, (m + 1) * M_TILE)
             if a == 0:
                 lhsT = x4_codes[:, 2 * m * M_TILE : 2 * (m + 1) * M_TILE].bitcast(E2M1X4)
@@ -115,11 +109,11 @@ def tile_mix_dwsav_none_kernel(tc, x4_words, x4_scales, x8, dy, out):
                 lhsT = stationary[a][1][:, cols].bitcast(E4M3X4)
                 lhsT_scale = stationary[a][2][:, cols]
             nc.tensor.matmul_mx(
-                out=bank[:],
+                out=bank,
                 lhsT=lhsT,
                 lhsT_scale=lhsT_scale,
-                rhs=moving[a][1][:, at : at + N_TILE].bitcast(E5M2X4),
-                rhs_scale=moving[a][2][:, at : at + N_TILE],
+                rhs=moving[a][1][:, at : at + width].bitcast(E5M2X4),
+                rhs_scale=moving[a][2][:, at : at + width],
                 start=start,
                 stop=stop,
             )
@@ -127,7 +121,7 @@ def tile_mix_dwsav_none_kernel(tc, x4_words, x4_scales, x8, dy, out):
         def multiply_mid(a):
             for m in range(M_TILES):
                 odd = m % 2
-                multiply(a, m, mid_bank[m // 2], MID_AT - odd * HALF, a == 0 and odd == 0, a == 2 and odd == 1)
+                multiply(a, m, block(mid_bank[m // 2], odd, HALF), MID_AT, a == 0 and odd == 0, a == 2 and odd == 1, HALF)
 
         def store(src, width, h0, m0, count):
             nc.sync.dma_start(
@@ -146,8 +140,8 @@ def tile_mix_dwsav_none_kernel(tc, x4_words, x4_scales, x8, dy, out):
                 in_=x4_scales[0, row : row + count, :].bitcast(I32),
             )
         x1 = load_x8(1)
-        nc.sync.dma_start(out=x4_codes[:].bitcast(I32), in_=x4_words[0].bitcast(I32))
         dy2_left = load_dy(2, 0, N_TILE)
+        nc.sync.dma_start(out=x4_codes[:].bitcast(I32), in_=x4_words[0].bitcast(I32))
         dy1_left = load_dy(1, 0, N_TILE)
         x2 = load_x8(2)
         dy1_mid = load_dy(1, MID_H, LAST_H)
@@ -178,23 +172,19 @@ def tile_mix_dwsav_none_kernel(tc, x4_words, x4_scales, x8, dy, out):
         quantize(stationary[1], E4M3X4, 0, D)
         prepare_left(dy2_left, 2, V_DY2)
 
-        for i, m in enumerate(borrowers):
-            multiply(0, m, mid_bank[i], LAST_WINDOW, True, True)
-        for i, m in enumerate(borrowers):
-            scalar(out=block(partial, m, HALF), in_=mid_bank[i][:, HALF:])
         for m in range(M_TILES):
-            multiply(0, m, left_bank[m], 0, True, False)
+            multiply(0, m, left_bank[m][:], 0, True, False)
         for m in OWN_BANK:
-            multiply(0, m, own_bank[m], LAST_WINDOW, True, False)
+            multiply(0, m, own_bank[m][:, HALF:], LAST_AT, True, False, HALF)
         multiply_mid(0)
 
         prepare_left(dy1_left, 1, V_DY1)
         for m in range(M_TILES):
-            multiply(1, m, left_bank[m], 0, False, False)
+            multiply(1, m, left_bank[m][:], 0, False, False)
 
         def finish_left(m):
             quantize(stationary[2], E4M3X4, m * M_TILE, M_TILE)
-            multiply(2, m, left_bank[m], 0, False, True)
+            multiply(2, m, left_bank[m][:], 0, False, True)
             scalar(out=block(left, m, N_TILE), in_=left_bank[m][:])
 
         for m in (2, 3):
@@ -220,22 +210,19 @@ def tile_mix_dwsav_none_kernel(tc, x4_words, x4_scales, x8, dy, out):
         store(mid, HALF, MID_H, 0, M_TILES)
 
         prepare_late(dy1_last, 1, LAST_AT, LATE_PARTS)
+        for m in borrowers:
+            multiply(0, m, last_bank[m][:, HALF:], LAST_AT, True, False, HALF)
         for m in range(M_TILES):
-            multiply(1, m, last_bank[m], LAST_WINDOW, m in borrowers, False)
+            multiply(1, m, last_bank[m][:, HALF:], LAST_AT, False, False, HALF)
         for i in range(2):
             interleave(vector, dy2_last[i], 0, moving[2], LAST_AT + i * QUARTER, QUARTER)
         for i in range(2):
             quantize_dy(2, LAST_AT + i * QUARTER, QUARTER)
+        for i in range(2):
+            for m in range(M_TILES):
+                part = block(last_bank[m], 2 + i, QUARTER)
+                multiply(2, m, part, LAST_AT + i * QUARTER, False, i == 1, QUARTER)
         for m in range(M_TILES):
-            multiply(2, m, last_bank[m], LAST_WINDOW, False, True)
-        for m in range(M_TILES):
-            if m in OWN_BANK:
-                scalar(out=block(last, m, HALF), in_=last_bank[m][:, HALF:])
-            else:
-                nc.vector.tensor_tensor(
-                    out=block(last, m, HALF),
-                    in0=last_bank[m][:, HALF:],
-                    in1=block(partial, m, HALF),
-                    op=mybir.AluOpType.add,
-                )
+            copy = scalar if m in OWN_BANK else vector
+            copy(out=block(last, m, HALF), in_=last_bank[m][:, HALF:])
             store(last, HALF, LAST_H, m, 1)

@@ -133,12 +133,11 @@ def tile_mix_dwsav_none_kernel(tc, x4_words, x4_scales, x8, dy, out):
             return tile[:, m * width : (m + 1) * width]
 
         dy0 = load_dy(0, 0, H)
-        for row, count in ((0, 2), (2, 2), (4, 4), (8, 4), (12, 4)):
-            at = 32 * (row // 4) + row % 4
-            nc.sync.dma_start(
-                out=x4_plane[at : at + count, :].bitcast(I32),
-                in_=x4_scales[0, row : row + count, :].bitcast(I32),
-            )
+        x4_rows = keep.tile([4, 4 * D], U8, name="x4_rows", align_bytes=ALIGN)
+        nc.sync.dma_start(
+            out=x4_rows[:].bitcast(I32).rearrange("r (q n) -> r q n", q=4),
+            in_=x4_scales[0].bitcast(I32).rearrange("(q r) n -> r q n", q=4),
+        )
         x1 = load_x8(1)
         dy2_left = load_dy(2, 0, N_TILE)
         nc.sync.dma_start(out=x4_codes[:].bitcast(I32), in_=x4_words[0].bitcast(I32))
@@ -169,6 +168,11 @@ def tile_mix_dwsav_none_kernel(tc, x4_words, x4_scales, x8, dy, out):
         quantize_dy(0, MID_AT, HALF)
         quantize_dy(0, LAST_AT, HALF)
         interleave_shared(x1, 0, stationary[1], D, V_EARLY)
+        for q in range(4):
+            vector(
+                out=x4_plane[32 * q : 32 * q + 4, :].bitcast(I32),
+                in_=x4_rows[:, q * D : (q + 1) * D].bitcast(I32),
+            )
         quantize(stationary[1], E4M3X4, 0, D)
         prepare_left(dy2_left, 2, V_DY2)
 
@@ -225,4 +229,4 @@ def tile_mix_dwsav_none_kernel(tc, x4_words, x4_scales, x8, dy, out):
         for m in range(M_TILES):
             copy = scalar if m in OWN_BANK else vector
             copy(out=block(last, m, HALF), in_=last_bank[m][:, HALF:])
-            store(last, HALF, LAST_H, m, 1)
+        store(last, HALF, LAST_H, 0, M_TILES)

@@ -20,6 +20,7 @@ N_TILE = 512
 M_TILES = D // M_TILE
 HALF = N_TILE // 2
 QUARTER = HALF // 2
+EIGHTH = QUARTER // 2
 MID_H = N_TILE
 LAST_H = N_TILE + HALF
 MID_AT = MID_H
@@ -27,13 +28,13 @@ LAST_AT = LAST_H
 DY_WORDS = H
 RUN = 4
 
-OWN_BANK = (1, 3)
 
 ALIGN = 256
 
 V_EARLY = 288
 V_DY2 = 320
-V_DY1 = 384
+V_X8 = 256
+V_FIRST = 160
 LATE_PARTS = (QUARTER, QUARTER)
 
 FLOPS = 2 * T * D * H
@@ -60,23 +61,19 @@ def tile_mix_dwsav_none_kernel(tc, x4_words, x4_scales, x8, dy, out):
         def load_dy(a, lo, hi):
             return load("dy%d_%d" % (a, lo), dy, a * K_PASS, lo, hi)
 
-        def load_x8(a):
-            return load("x8_%d" % a, x8, (a - 1) * K_PASS, 0, D)
-
         def operand(name, width, codes_at, plane_at):
             grouped = keep.tile([P, PACK * width], BF16, name="grouped_" + name, align_bytes=ALIGN)
             codes = keep.tile([P, width + ALIGN // 4], U32, name="codes_" + name, align_bytes=ALIGN)
             plane = keep.tile([P, width + ALIGN], U8, name="plane_" + name, align_bytes=ALIGN)
             return grouped, codes[:, codes_at // 4 : codes_at // 4 + width], plane[:, plane_at : plane_at + width]
 
-        left = keep.tile([M_TILE, M_TILES * N_TILE], F32, name="left", align_bytes=ALIGN)
+        left = [keep.tile([M_TILE, M_TILES * HALF], F32, name="left%d" % i, align_bytes=ALIGN) for i in range(2)]
         mid = keep.tile([M_TILE, M_TILES * HALF], F32, name="mid", align_bytes=ALIGN)
-        last = keep.tile([M_TILE, M_TILES * HALF], F32, name="last", align_bytes=ALIGN)
+        last = [keep.tile([M_TILE, M_TILES * QUARTER], F32, name="last%d" % i, align_bytes=ALIGN) for i in range(2)]
         left_bank = [psum.tile([M_TILE, N_TILE], F32, name="left_bank%d" % m) for m in range(M_TILES)]
         mid_bank = [psum.tile([M_TILE, N_TILE], F32, name="mid_bank%d" % i) for i in range(M_TILES // 2)]
-        own_bank = {m: psum.tile([M_TILE, N_TILE], F32, name="own_bank%d" % m) for m in OWN_BANK}
-        borrowers = [m for m in range(M_TILES) if m not in OWN_BANK]
-        last_bank = [own_bank.get(m, left_bank[m]) for m in range(M_TILES)]
+        own_bank = [psum.tile([M_TILE, N_TILE], F32, name="own_bank%d" % i) for i in range(2)]
+        last_bank = [(own_bank[i], left_bank[i]) for i in range(2)]
         moving = {a: operand("dy%d" % a, DY_WORDS, 0, 128) for a in range(3)}
         stationary = {a: operand("x8_%d" % a, D, 64, 192) for a in (1, 2)}
 
@@ -123,6 +120,12 @@ def tile_mix_dwsav_none_kernel(tc, x4_words, x4_scales, x8, dy, out):
                 odd = m % 2
                 multiply(a, m, block(mid_bank[m // 2], odd, HALF), MID_AT, a == 0 and odd == 0, a == 2 and odd == 1, HALF)
 
+        def multiply_last(a, part, pair):
+            for odd in range(2):
+                bank = block(last_bank[part][pair], odd, QUARTER)
+                at = LAST_AT + part * QUARTER
+                multiply(a, 2 * pair + odd, bank, at, a == 0 and odd == 0, a == 2 and odd == 1, QUARTER)
+
         def store(src, width, h0, m0, count):
             nc.sync.dma_start(
                 out=out[m0 * M_TILE : (m0 + count) * M_TILE, h0 : h0 + width].rearrange("(i p) h -> p i h", i=count),
@@ -138,21 +141,19 @@ def tile_mix_dwsav_none_kernel(tc, x4_words, x4_scales, x8, dy, out):
             out=x4_rows[:].bitcast(I32).rearrange("r (q n) -> r q n", q=4),
             in_=x4_scales[0].bitcast(I32).rearrange("(q r) n -> r q n", q=4),
         )
-        x1 = load_x8(1)
-        dy2_left = load_dy(2, 0, N_TILE)
+        x_raw = keep.tile([P, 2 * PACK, D], F32, name="x_raw", align_bytes=ALIGN)
+        nc.sync.dma_start(
+            out=x_raw[:].rearrange("p (a j) w -> p a (j w)", a=2),
+            in_=x8.rearrange("(a p j) w -> p a (j w)", a=2, j=PACK),
+        )
+        x1, x2 = x_raw[:, :PACK, :], x_raw[:, PACK:, :]
         nc.sync.dma_start(out=x4_codes[:].bitcast(I32), in_=x4_words[0].bitcast(I32))
+        dy2_left = load_dy(2, 0, N_TILE)
         dy1_left = load_dy(1, 0, N_TILE)
-        x2 = load_x8(2)
         dy1_mid = load_dy(1, MID_H, LAST_H)
         dy2_mid = load_dy(2, MID_H, LAST_H)
         dy1_last = load_dy(1, LAST_H, H)
         dy2_last = [load_dy(2, LAST_H + i * QUARTER, LAST_H + (i + 1) * QUARTER) for i in range(2)]
-
-        def prepare_left(raw, a, v_cols):
-            interleave(vector, raw, 0, moving[a], 0, HALF)
-            interleave_shared(raw, HALF, moving[a], HALF, v_cols - HALF)
-            quantize_dy(a, 0, HALF)
-            quantize_dy(a, HALF, HALF)
 
         def prepare_late(raw, a, at0, parts):
             starts = [sum(parts[:i]) for i in range(len(parts))]
@@ -167,45 +168,47 @@ def tile_mix_dwsav_none_kernel(tc, x4_words, x4_scales, x8, dy, out):
         quantize_dy(0, 0, N_TILE)
         quantize_dy(0, MID_AT, HALF)
         quantize_dy(0, LAST_AT, HALF)
-        interleave_shared(x1, 0, stationary[1], D, V_EARLY)
         for q in range(4):
             vector(
                 out=x4_plane[32 * q : 32 * q + 4, :].bitcast(I32),
                 in_=x4_rows[:, q * D : (q + 1) * D].bitcast(I32),
             )
+        interleave_shared(x2, 0, stationary[2], D, V_X8)
+        interleave_shared(x1, 0, stationary[1], D, V_X8)
+        quantize(stationary[2], E4M3X4, 0, D)
         quantize(stationary[1], E4M3X4, 0, D)
-        prepare_left(dy2_left, 2, V_DY2)
+        interleave(vector, dy2_left, 0, moving[2], 0, HALF)
+        interleave_shared(dy2_left, HALF, moving[2], HALF, V_DY2 - HALF)
+        quantize_dy(2, 0, HALF)
+        quantize_dy(2, HALF, HALF)
 
-        for m in range(M_TILES):
-            multiply(0, m, left_bank[m][:], 0, True, False)
-        for m in OWN_BANK:
-            multiply(0, m, own_bank[m][:, HALF:], LAST_AT, True, False, HALF)
+        def multiply_left(a, half):
+            for m in range(M_TILES):
+                odd = m % 2
+                bank = block(left_bank[2 * half + m // 2], odd, HALF)
+                multiply(a, m, bank, half * HALF, a == 0 and odd == 0, a == 1 and odd == 1, HALF)
+
+        for half in range(2):
+            multiply_left(0, half)
+        for part in range(2):
+            multiply_last(0, part, 0)
         multiply_mid(0)
+        for half in range(2):
+            multiply_left(2, half)
 
-        prepare_left(dy1_left, 1, V_DY1)
-        for m in range(M_TILES):
-            multiply(1, m, left_bank[m][:], 0, False, False)
-
-        def finish_left(m):
-            quantize(stationary[2], E4M3X4, m * M_TILE, M_TILE)
-            multiply(2, m, left_bank[m][:], 0, False, True)
-            scalar(out=block(left, m, N_TILE), in_=left_bank[m][:])
-
-        for m in (2, 3):
-            interleave(scalar, x2, m * M_TILE, stationary[2], m * M_TILE, M_TILE)
+        interleave_shared(dy1_left, 0, moving[1], HALF, V_FIRST)
+        interleave_shared(dy1_left, HALF, moving[1], HALF, QUARTER)
         interleave(scalar, dy1_mid, QUARTER, moving[1], MID_AT + QUARTER, QUARTER)
-        for m in (0, 1):
-            interleave(vector, x2, m * M_TILE, stationary[2], m * M_TILE, M_TILE)
-        finish_left(0)
-        finish_left(1)
-        store(left, N_TILE, 0, 0, 2)
-        finish_left(2)
+        for half in range(2):
+            quantize_dy(1, half * HALF, HALF)
+            multiply_left(1, half)
+            for pair in range(2):
+                scalar(out=block(left[half], pair, N_TILE), in_=left_bank[2 * half + pair][:])
+            store(left[half], HALF, half * HALF, 0, M_TILES)
         interleave(vector, dy1_mid, 0, moving[1], MID_AT, QUARTER)
-        finish_left(3)
-        store(left, N_TILE, 0, 2, 2)
 
         for i in range(2):
-            quantize_dy(1, MID_AT + i * QUARTER, QUARTER)
+            quantize_dy(1, MID_AT + (1 - i) * QUARTER, QUARTER)
         multiply_mid(1)
         prepare_late(dy2_mid, 2, MID_AT, LATE_PARTS)
         multiply_mid(2)
@@ -213,20 +216,21 @@ def tile_mix_dwsav_none_kernel(tc, x4_words, x4_scales, x8, dy, out):
             scalar(out=block(mid, i, N_TILE), in_=mid_bank[i][:])
         store(mid, HALF, MID_H, 0, M_TILES)
 
-        prepare_late(dy1_last, 1, LAST_AT, LATE_PARTS)
-        for m in borrowers:
-            multiply(0, m, last_bank[m][:, HALF:], LAST_AT, True, False, HALF)
-        for m in range(M_TILES):
-            multiply(1, m, last_bank[m][:, HALF:], LAST_AT, False, False, HALF)
+        interleave(vector, dy1_last, 0, moving[1], LAST_AT, HALF)
+        interleave(vector, dy2_last[0], 0, moving[2], LAST_AT, QUARTER)
+        quantize_dy(1, LAST_AT, HALF)
+        quantize_dy(2, LAST_AT, QUARTER)
         for i in range(2):
-            interleave(vector, dy2_last[i], 0, moving[2], LAST_AT + i * QUARTER, QUARTER)
+            interleave(vector, dy2_last[1], i * EIGHTH, moving[2], LAST_AT + QUARTER + i * EIGHTH, EIGHTH)
         for i in range(2):
-            quantize_dy(2, LAST_AT + i * QUARTER, QUARTER)
-        for i in range(2):
-            for m in range(M_TILES):
-                part = block(last_bank[m], 2 + i, QUARTER)
-                multiply(2, m, part, LAST_AT + i * QUARTER, False, i == 1, QUARTER)
-        for m in range(M_TILES):
-            copy = scalar if m in OWN_BANK else vector
-            copy(out=block(last, m, HALF), in_=last_bank[m][:, HALF:])
-        store(last, HALF, LAST_H, 0, M_TILES)
+            quantize_dy(2, LAST_AT + QUARTER + i * EIGHTH, EIGHTH)
+        for part in range(2):
+            multiply_last(0, part, 1)
+        for part in range(2):
+            for a in (1, 2):
+                for pair in range(2):
+                    multiply_last(a, part, pair)
+            for pair in range(2):
+                copy = vector if part == 1 and pair == 1 else scalar
+                copy(out=block(last[part], pair, HALF), in_=last_bank[part][pair][:, :HALF])
+            store(last[part], QUARTER, LAST_H + part * QUARTER, 0, M_TILES)

@@ -20,7 +20,7 @@ N_TILE = 512
 M_TILES = D // M_TILE
 HALF = N_TILE // 2
 QUARTER = HALF // 2
-EIGHTH = QUARTER // 2
+BORROWERS = (0, 2)
 MID_H = N_TILE
 LAST_H = N_TILE + HALF
 MID_AT = MID_H
@@ -32,8 +32,8 @@ RUN = 4
 ALIGN = 256
 
 V_EARLY = 288
-V_DY2 = 320
-V_X8 = 256
+V_DY2 = 288
+V_X8 = 288
 V_FIRST = 160
 LATE_PARTS = (QUARTER, QUARTER)
 
@@ -69,11 +69,11 @@ def tile_mix_dwsav_none_kernel(tc, x4_words, x4_scales, x8, dy, out):
 
         left = [keep.tile([M_TILE, M_TILES * HALF], F32, name="left%d" % i, align_bytes=ALIGN) for i in range(2)]
         mid = keep.tile([M_TILE, M_TILES * HALF], F32, name="mid", align_bytes=ALIGN)
-        last = [keep.tile([M_TILE, M_TILES * QUARTER], F32, name="last%d" % i, align_bytes=ALIGN) for i in range(2)]
+        last = keep.tile([M_TILE, M_TILES * HALF], F32, name="last", align_bytes=ALIGN)
         left_bank = [psum.tile([M_TILE, N_TILE], F32, name="left_bank%d" % m) for m in range(M_TILES)]
         mid_bank = [psum.tile([M_TILE, N_TILE], F32, name="mid_bank%d" % i) for i in range(M_TILES // 2)]
         own_bank = [psum.tile([M_TILE, N_TILE], F32, name="own_bank%d" % i) for i in range(2)]
-        last_bank = [(own_bank[i], left_bank[i]) for i in range(2)]
+        last_bank = [left_bank[0], own_bank[0], left_bank[1], own_bank[1]]
         moving = {a: operand("dy%d" % a, DY_WORDS, 0, 128) for a in range(3)}
         stationary = {a: operand("x8_%d" % a, D, 64, 192) for a in (1, 2)}
 
@@ -119,12 +119,6 @@ def tile_mix_dwsav_none_kernel(tc, x4_words, x4_scales, x8, dy, out):
             for m in range(M_TILES):
                 odd = m % 2
                 multiply(a, m, block(mid_bank[m // 2], odd, HALF), MID_AT, a == 0 and odd == 0, a == 2 and odd == 1, HALF)
-
-        def multiply_last(a, part, pair):
-            for odd in range(2):
-                bank = block(last_bank[part][pair], odd, QUARTER)
-                at = LAST_AT + part * QUARTER
-                multiply(a, 2 * pair + odd, bank, at, a == 0 and odd == 0, a == 2 and odd == 1, QUARTER)
 
         def store(src, width, h0, m0, count):
             nc.sync.dma_start(
@@ -190,8 +184,9 @@ def tile_mix_dwsav_none_kernel(tc, x4_words, x4_scales, x8, dy, out):
 
         for half in range(2):
             multiply_left(0, half)
-        for part in range(2):
-            multiply_last(0, part, 0)
+        for m in range(M_TILES):
+            if m not in BORROWERS:
+                multiply(0, m, last_bank[m][:, :HALF], LAST_AT, True, False, HALF)
         multiply_mid(0)
         for half in range(2):
             multiply_left(2, half)
@@ -216,21 +211,21 @@ def tile_mix_dwsav_none_kernel(tc, x4_words, x4_scales, x8, dy, out):
             scalar(out=block(mid, i, N_TILE), in_=mid_bank[i][:])
         store(mid, HALF, MID_H, 0, M_TILES)
 
-        interleave(vector, dy1_last, 0, moving[1], LAST_AT, HALF)
-        interleave(vector, dy2_last[0], 0, moving[2], LAST_AT, QUARTER)
-        quantize_dy(1, LAST_AT, HALF)
-        quantize_dy(2, LAST_AT, QUARTER)
+        prepare_late(dy1_last, 1, LAST_AT, LATE_PARTS)
+        for m in BORROWERS:
+            multiply(0, m, last_bank[m][:, :HALF], LAST_AT, True, False, HALF)
+        for m in range(M_TILES):
+            multiply(1, m, last_bank[m][:, :HALF], LAST_AT, False, False, HALF)
         for i in range(2):
-            interleave(vector, dy2_last[1], i * EIGHTH, moving[2], LAST_AT + QUARTER + i * EIGHTH, EIGHTH)
+            interleave(vector, dy2_last[i], 0, moving[2], LAST_AT + i * QUARTER, QUARTER)
         for i in range(2):
-            quantize_dy(2, LAST_AT + QUARTER + i * EIGHTH, EIGHTH)
-        for part in range(2):
-            multiply_last(0, part, 1)
-        for part in range(2):
-            for a in (1, 2):
-                for pair in range(2):
-                    multiply_last(a, part, pair)
-            for pair in range(2):
-                copy = vector if part == 1 and pair == 1 else scalar
-                copy(out=block(last[part], pair, HALF), in_=last_bank[part][pair][:, :HALF])
-            store(last[part], QUARTER, LAST_H + part * QUARTER, 0, M_TILES)
+            quantize_dy(2, LAST_AT + i * QUARTER, QUARTER)
+        for i in range(2):
+            for m in range(M_TILES):
+                part = block(last_bank[m], i, QUARTER)
+                multiply(2, m, part, LAST_AT + i * QUARTER, False, i == 1, QUARTER)
+        for m in range(M_TILES):
+            copy = vector if m in BORROWERS else scalar
+            copy(out=block(last, m, HALF), in_=last_bank[m][:, :HALF])
+            if m % 2 == 1:
+                store(last, HALF, LAST_H, m - 1, 2)

@@ -147,7 +147,7 @@ def tile_mix_dwsav_none_kernel(tc, x4_words, x4_scales, x8, dy, out):
         dy1_mid = load_dy(1, MID_H, LAST_H)
         dy2_mid = load_dy(2, MID_H, LAST_H)
         dy1_last = load_dy(1, LAST_H, H)
-        dy2_last = [load_dy(2, LAST_H + i * QUARTER, LAST_H + (i + 1) * QUARTER) for i in range(2)]
+        dy2_last = load_dy(2, LAST_H, H)
 
         def prepare_late(raw, a, at0, parts):
             starts = [sum(parts[:i]) for i in range(len(parts))]
@@ -216,10 +216,7 @@ def tile_mix_dwsav_none_kernel(tc, x4_words, x4_scales, x8, dy, out):
             multiply(0, m, last_bank[m][:, :HALF], LAST_AT, True, False, HALF)
         for m in range(M_TILES):
             multiply(1, m, last_bank[m][:, :HALF], LAST_AT, False, False, HALF)
-        for i in range(2):
-            interleave(vector, dy2_last[i], 0, moving[2], LAST_AT + i * QUARTER, QUARTER)
-        for i in range(2):
-            quantize_dy(2, LAST_AT + i * QUARTER, QUARTER)
+        prepare_late(dy2_last, 2, LAST_AT, LATE_PARTS)
         for i in range(2):
             for m in range(M_TILES):
                 part = block(last_bank[m], i, QUARTER)

@@ -16,26 +16,19 @@ P = 128
 PACK = 4
 K_PASS = P * PACK
 M_TILE = 128
-N_TILE = 512
 M_TILES = D // M_TILE
-HALF = N_TILE // 2
-QUARTER = HALF // 2
-BORROWERS = (0, 2)
-MID_H = N_TILE
-LAST_H = N_TILE + HALF
-MID_AT = MID_H
-LAST_AT = LAST_H
-DY_WORDS = H
+BANK = 512
+LEFT = BANK
+NARROW = LEFT // 2
+MID = LEFT
+LAST = MID + NARROW
+PART = NARROW // 2
+QUADRANTS, QUADRANT, SCALE_ROWS = 4, 32, 4
 RUN = 4
-
 
 ALIGN = 256
 
-V_EARLY = 288
-V_DY2 = 288
-V_X8 = 288
 V_FIRST = 160
-LATE_PARTS = (QUARTER, QUARTER)
 
 FLOPS = 2 * T * D * H
 
@@ -52,14 +45,11 @@ def tile_mix_dwsav_none_kernel(tc, x4_words, x4_scales, x8, dy, out):
         x4_plane = keep.tile([P, D], U8, name="x4_plane", align_bytes=ALIGN)
         nc.vector.memset(x4_plane[:].bitcast(I32), 0)
 
-        def load(name, src, row0, lo, hi):
-            raw = keep.tile([P, PACK, hi - lo], F32, name="raw_" + name, align_bytes=ALIGN)
-            rows = src[row0 : row0 + K_PASS, lo:hi]
+        def load_dy(a, lo, hi):
+            raw = keep.tile([P, PACK, hi - lo], F32, name="raw_dy%d_%d" % (a, lo), align_bytes=ALIGN)
+            rows = dy[a * K_PASS : (a + 1) * K_PASS, lo:hi]
             nc.sync.dma_start(out=raw[:], in_=rows.rearrange("(p j) w -> p j w", j=PACK))
             return raw
-
-        def load_dy(a, lo, hi):
-            return load("dy%d_%d" % (a, lo), dy, a * K_PASS, lo, hi)
 
         def operand(name, width, codes_at, plane_at):
             grouped = keep.tile([P, PACK * width], BF16, name="grouped_" + name, align_bytes=ALIGN)
@@ -67,25 +57,21 @@ def tile_mix_dwsav_none_kernel(tc, x4_words, x4_scales, x8, dy, out):
             plane = keep.tile([P, width + ALIGN], U8, name="plane_" + name, align_bytes=ALIGN)
             return grouped, codes[:, codes_at // 4 : codes_at // 4 + width], plane[:, plane_at : plane_at + width]
 
-        left = [keep.tile([M_TILE, M_TILES * HALF], F32, name="left%d" % i, align_bytes=ALIGN) for i in range(2)]
-        mid = keep.tile([M_TILE, M_TILES * HALF], F32, name="mid", align_bytes=ALIGN)
-        last = keep.tile([M_TILE, M_TILES * HALF], F32, name="last", align_bytes=ALIGN)
-        left_bank = [psum.tile([M_TILE, N_TILE], F32, name="left_bank%d" % m) for m in range(M_TILES)]
-        mid_bank = [psum.tile([M_TILE, N_TILE], F32, name="mid_bank%d" % i) for i in range(M_TILES // 2)]
-        own_bank = [psum.tile([M_TILE, N_TILE], F32, name="own_bank%d" % i) for i in range(2)]
-        last_bank = [left_bank[0], own_bank[0], left_bank[1], own_bank[1]]
-        moving = {a: operand("dy%d" % a, DY_WORDS, 0, 128) for a in range(3)}
+        left = [keep.tile([M_TILE, M_TILES * NARROW], F32, name="left%d" % i, align_bytes=ALIGN) for i in range(2)]
+        mid = keep.tile([M_TILE, M_TILES * NARROW], F32, name="mid", align_bytes=ALIGN)
+        last = keep.tile([M_TILE, M_TILES * NARROW], F32, name="last", align_bytes=ALIGN)
+        left_bank = [psum.tile([M_TILE, BANK], F32, name="left_bank%d" % m) for m in range(M_TILES)]
+        mid_bank = [psum.tile([M_TILE, BANK], F32, name="mid_bank%d" % pair) for pair in range(2)]
+        last_bank = [psum.tile([M_TILE, BANK], F32, name="last_bank%d" % m) for m in range(2)] + left_bank[:2]
+        moving = {a: operand("dy%d" % a, H, 0, 128) for a in (1, 2)}
+        moving[0] = operand("dy0", H, 64, 192)
         stationary = {a: operand("x8_%d" % a, D, 64, 192) for a in (1, 2)}
 
-        def interleave(copy, raw, lo, op, at, width):
+        def interleave(copy, raw, lo, hi, op, at):
             copy(
-                out=op[0][:, PACK * at : PACK * (at + width)].rearrange("p (c i j) -> p c j i", i=RUN, j=PACK),
-                in_=raw[:, :, lo : lo + width].rearrange("p j (c i) -> p c j i", i=RUN),
+                out=op[0][:, PACK * (at + lo) : PACK * (at + hi)].rearrange("p (c i j) -> p c j i", i=RUN, j=PACK),
+                in_=raw[:, :, lo:hi].rearrange("p j (c i) -> p c j i", i=RUN),
             )
-
-        def interleave_shared(raw, lo, op, width, v_cols):
-            interleave(vector, raw, lo, op, lo, v_cols)
-            interleave(scalar, raw, lo + v_cols, op, lo + v_cols, width - v_cols)
 
         def quantize(op, fmt, at, width):
             nc.vector.quantize_mx(
@@ -94,10 +80,19 @@ def tile_mix_dwsav_none_kernel(tc, x4_words, x4_scales, x8, dy, out):
                 in_=op[0][:, PACK * at : PACK * (at + width)],
             )
 
+        def copy_dy(copy, raw, a, at, lo, hi):
+            interleave(copy, raw, lo, hi, moving[a], at)
+
         def quantize_dy(a, at, width):
             quantize(moving[a], E5M2X4, at, width)
 
-        def multiply(a, m, bank, at, start, stop, width=N_TILE):
+        def prepare_alone(raw, a, at):
+            for i in range(2):
+                copy_dy(vector, raw, a, at, i * PART, (i + 1) * PART)
+            for i in range(2):
+                quantize_dy(a, at + i * PART, PART)
+
+        def multiply(a, m, bank, at, lo, width, start, stop):
             cols = slice(m * M_TILE, (m + 1) * M_TILE)
             if a == 0:
                 lhsT = x4_codes[:, 2 * m * M_TILE : 2 * (m + 1) * M_TILE].bitcast(E2M1X4)
@@ -106,123 +101,117 @@ def tile_mix_dwsav_none_kernel(tc, x4_words, x4_scales, x8, dy, out):
                 lhsT = stationary[a][1][:, cols].bitcast(E4M3X4)
                 lhsT_scale = stationary[a][2][:, cols]
             nc.tensor.matmul_mx(
-                out=bank,
+                out=bank[:, lo : lo + width],
                 lhsT=lhsT,
                 lhsT_scale=lhsT_scale,
-                rhs=moving[a][1][:, at : at + width].bitcast(E5M2X4),
-                rhs_scale=moving[a][2][:, at : at + width],
+                rhs=moving[a][1][:, at + lo : at + lo + width].bitcast(E5M2X4),
+                rhs_scale=moving[a][2][:, at + lo : at + lo + width],
                 start=start,
                 stop=stop,
             )
 
-        def multiply_mid(a):
+        def paired_pass(a, banks, at, first, closing):
             for m in range(M_TILES):
                 odd = m % 2
-                multiply(a, m, block(mid_bank[m // 2], odd, HALF), MID_AT, a == 0 and odd == 0, a == 2 and odd == 1, HALF)
+                multiply(a, m, banks[m // 2][:, odd * NARROW :], at, 0, NARROW, first and not odd, closing and odd == 1)
 
-        def store(src, width, h0, m0, count):
+        def left_pass(a, half, first, closing):
+            paired_pass(a, left_bank[2 * half : 2 * half + 2], half * NARROW, first, closing)
+
+        def last_pass(a, blocks):
+            for m in blocks:
+                multiply(a, m, last_bank[m], LAST, 0, NARROW, a == 0, False)
+
+        def close(sums, at, stops):
+            for i in range(2):
+                for m in range(2):
+                    multiply(2, m, sums[m], at, i * PART, PART, False, i == 1 and m in stops)
+            for m in range(2, M_TILES):
+                multiply(2, m, sums[m], at, 0, NARROW, False, m in stops)
+
+        def store(staged, h0, m0, count):
             nc.sync.dma_start(
-                out=out[m0 * M_TILE : (m0 + count) * M_TILE, h0 : h0 + width].rearrange("(i p) h -> p i h", i=count),
-                in_=src[:, m0 * width : (m0 + count) * width].rearrange("p (i h) -> p i h", i=count),
+                out=out[m0 * M_TILE : (m0 + count) * M_TILE, h0 : h0 + NARROW].rearrange("(i p) h -> p i h", i=count),
+                in_=staged[:, m0 * NARROW : (m0 + count) * NARROW].rearrange("p (i h) -> p i h", i=count),
             )
 
-        def block(tile, m, width):
-            return tile[:, m * width : (m + 1) * width]
+        def empty_pairs(staged, banks, h0):
+            for pair in range(2):
+                scalar(out=staged[:, pair * BANK : (pair + 1) * BANK], in_=banks[pair][:])
+            store(staged, h0, 0, M_TILES)
 
         dy0 = load_dy(0, 0, H)
-        x4_rows = keep.tile([4, 4 * D], U8, name="x4_rows", align_bytes=ALIGN)
+        x4_rows = keep.tile([SCALE_ROWS, QUADRANTS * D], U8, name="x4_rows", align_bytes=ALIGN)
         nc.sync.dma_start(
-            out=x4_rows[:].bitcast(I32).rearrange("r (q n) -> r q n", q=4),
-            in_=x4_scales[0].bitcast(I32).rearrange("(q r) n -> r q n", q=4),
+            out=x4_rows[:].bitcast(I32).rearrange("r (q n) -> r q n", q=QUADRANTS),
+            in_=x4_scales[0].bitcast(I32).rearrange("(q r) n -> r q n", q=QUADRANTS),
         )
         x_raw = keep.tile([P, 2 * PACK, D], F32, name="x_raw", align_bytes=ALIGN)
         nc.sync.dma_start(
             out=x_raw[:].rearrange("p (a j) w -> p a (j w)", a=2),
             in_=x8.rearrange("(a p j) w -> p a (j w)", a=2, j=PACK),
         )
-        x1, x2 = x_raw[:, :PACK, :], x_raw[:, PACK:, :]
         nc.sync.dma_start(out=x4_codes[:].bitcast(I32), in_=x4_words[0].bitcast(I32))
-        dy2_left = load_dy(2, 0, N_TILE)
-        dy1_left = load_dy(1, 0, N_TILE)
-        dy1_mid = load_dy(1, MID_H, LAST_H)
-        dy2_mid = load_dy(2, MID_H, LAST_H)
-        dy1_last = load_dy(1, LAST_H, H)
-        dy2_last = load_dy(2, LAST_H, H)
+        dy2_left = load_dy(2, 0, LEFT)
+        dy1_left = load_dy(1, 0, LEFT)
+        dy1_mid = load_dy(1, MID, LAST)
+        dy2_mid = load_dy(2, MID, LAST)
+        dy1_last = load_dy(1, LAST, H)
+        dy2_last = load_dy(2, LAST, H)
 
-        def prepare_late(raw, a, at0, parts):
-            starts = [sum(parts[:i]) for i in range(len(parts))]
-            for at, width in zip(starts, parts):
-                interleave(vector, raw, at, moving[a], at0 + at, width)
-            for at, width in zip(starts, parts):
-                quantize_dy(a, at0 + at, width)
-
-        interleave_shared(dy0, 0, moving[0], N_TILE, V_EARLY)
-        interleave(vector, dy0, MID_H, moving[0], MID_AT, HALF)
-        interleave(scalar, dy0, LAST_H, moving[0], LAST_AT, HALF)
-        quantize_dy(0, 0, N_TILE)
-        quantize_dy(0, MID_AT, HALF)
-        quantize_dy(0, LAST_AT, HALF)
-        for q in range(4):
+        for lo in (0, MID):
+            copy_dy(vector, dy0, 0, 0, lo, lo + NARROW)
+            copy_dy(scalar, dy0, 0, 0, lo + NARROW, lo + LEFT)
+        quantize_dy(0, 0, LEFT)
+        for q in range(QUADRANTS):
             vector(
-                out=x4_plane[32 * q : 32 * q + 4, :].bitcast(I32),
+                out=x4_plane[QUADRANT * q : QUADRANT * q + SCALE_ROWS, :].bitcast(I32),
                 in_=x4_rows[:, q * D : (q + 1) * D].bitcast(I32),
             )
-        interleave_shared(x2, 0, stationary[2], D, V_X8)
-        interleave_shared(x1, 0, stationary[1], D, V_X8)
+        quantize_dy(0, MID, H - MID)
+        for half in range(2):
+            left_pass(0, half, True, False)
+        paired_pass(0, mid_bank, MID, True, False)
+        last_pass(0, range(2))
+
+        for a in (2, 1):
+            rows = x_raw[:, (a - 1) * PACK : a * PACK, :]
+            interleave(vector, rows, 0, D // 2, stationary[a], 0)
+            interleave(scalar, rows, D // 2, D, stationary[a], 0)
         quantize(stationary[2], E4M3X4, 0, D)
+        copy_dy(vector, dy2_left, 2, 0, 0, NARROW)
+        copy_dy(scalar, dy2_left, 2, 0, NARROW, LEFT)
         quantize(stationary[1], E4M3X4, 0, D)
-        interleave(vector, dy2_left, 0, moving[2], 0, HALF)
-        interleave_shared(dy2_left, HALF, moving[2], HALF, V_DY2 - HALF)
-        quantize_dy(2, 0, HALF)
-        quantize_dy(2, HALF, HALF)
-
-        def multiply_left(a, half):
-            for m in range(M_TILES):
-                odd = m % 2
-                bank = block(left_bank[2 * half + m // 2], odd, HALF)
-                multiply(a, m, bank, half * HALF, a == 0 and odd == 0, a == 1 and odd == 1, HALF)
-
         for half in range(2):
-            multiply_left(0, half)
-        for m in range(M_TILES):
-            if m not in BORROWERS:
-                multiply(0, m, last_bank[m][:, :HALF], LAST_AT, True, False, HALF)
-        multiply_mid(0)
+            quantize_dy(2, half * NARROW, NARROW)
+            left_pass(2, half, False, False)
+
+        copy_dy(vector, dy1_left, 1, 0, 0, V_FIRST)
+        copy_dy(scalar, dy1_left, 1, 0, V_FIRST, NARROW)
+        copy_dy(vector, dy1_left, 1, 0, NARROW, LEFT - V_FIRST)
+        copy_dy(scalar, dy1_left, 1, 0, LEFT - V_FIRST, LEFT)
+        copy_dy(scalar, dy1_mid, 1, MID, PART, NARROW)
+        quantize_dy(1, 0, NARROW)
+        copy_dy(vector, dy1_mid, 1, MID, 0, PART)
+        quantize_dy(1, NARROW, NARROW)
         for half in range(2):
-            multiply_left(2, half)
+            left_pass(1, half, False, True)
+            empty_pairs(left[half], left_bank[2 * half : 2 * half + 2], half * NARROW)
 
-        interleave_shared(dy1_left, 0, moving[1], HALF, V_FIRST)
-        interleave_shared(dy1_left, HALF, moving[1], HALF, QUARTER)
-        interleave(scalar, dy1_mid, QUARTER, moving[1], MID_AT + QUARTER, QUARTER)
-        for half in range(2):
-            quantize_dy(1, half * HALF, HALF)
-            multiply_left(1, half)
-            for pair in range(2):
-                scalar(out=block(left[half], pair, N_TILE), in_=left_bank[2 * half + pair][:])
-            store(left[half], HALF, half * HALF, 0, M_TILES)
-        interleave(vector, dy1_mid, 0, moving[1], MID_AT, QUARTER)
+        quantize_dy(1, MID, NARROW)
+        paired_pass(1, mid_bank, MID, False, False)
+        prepare_alone(dy2_mid, 2, MID)
+        close([mid_bank[m // 2][:, m % 2 * NARROW :] for m in range(M_TILES)], MID, (1, 3))
+        empty_pairs(mid, mid_bank, MID)
 
-        for i in range(2):
-            quantize_dy(1, MID_AT + (1 - i) * QUARTER, QUARTER)
-        multiply_mid(1)
-        prepare_late(dy2_mid, 2, MID_AT, LATE_PARTS)
-        multiply_mid(2)
-        for i in range(M_TILES // 2):
-            scalar(out=block(mid, i, N_TILE), in_=mid_bank[i][:])
-        store(mid, HALF, MID_H, 0, M_TILES)
+        last_pass(0, range(2, M_TILES))
+        prepare_alone(dy1_last, 1, LAST)
+        last_pass(1, range(M_TILES))
+        prepare_alone(dy2_last, 2, LAST)
+        close(last_bank, LAST, range(M_TILES))
 
-        prepare_late(dy1_last, 1, LAST_AT, LATE_PARTS)
-        for m in BORROWERS:
-            multiply(0, m, last_bank[m][:, :HALF], LAST_AT, True, False, HALF)
         for m in range(M_TILES):
-            multiply(1, m, last_bank[m][:, :HALF], LAST_AT, False, False, HALF)
-        prepare_late(dy2_last, 2, LAST_AT, LATE_PARTS)
-        for i in range(2):
-            for m in range(M_TILES):
-                part = block(last_bank[m], i, QUARTER)
-                multiply(2, m, part, LAST_AT + i * QUARTER, False, i == 1, QUARTER)
-        for m in range(M_TILES):
-            copy = vector if m in BORROWERS else scalar
-            copy(out=block(last, m, HALF), in_=last_bank[m][:, :HALF])
-            if m % 2 == 1:
-                store(last, HALF, LAST_H, m - 1, 2)
+            copy = scalar if m % 2 else vector
+            copy(out=last[:, m * NARROW : (m + 1) * NARROW], in_=last_bank[m][:, :NARROW])
+            if m % 2:
+                store(last, LAST, m - 1, 2)

@@ -28,6 +28,7 @@ RUN = 4
 
 ALIGN = 256
 
+V_WIDE = 288
 V_FIRST = 160
 
 FLOPS = 2 * T * D * H
@@ -62,9 +63,9 @@ def tile_mix_dwsav_none_kernel(tc, x4_words, x4_scales, x8, dy, out):
         last = keep.tile([M_TILE, M_TILES * NARROW], F32, name="last", align_bytes=ALIGN)
         left_bank = [psum.tile([M_TILE, BANK], F32, name="left_bank%d" % m) for m in range(M_TILES)]
         mid_bank = [psum.tile([M_TILE, BANK], F32, name="mid_bank%d" % pair) for pair in range(2)]
-        last_bank = [psum.tile([M_TILE, BANK], F32, name="last_bank%d" % m) for m in range(2)] + left_bank[:2]
-        moving = {a: operand("dy%d" % a, H, 0, 128) for a in (1, 2)}
-        moving[0] = operand("dy0", H, 64, 192)
+        own_bank = [psum.tile([M_TILE, BANK], F32, name="own_bank%d" % i) for i in range(2)]
+        last_bank = [left_bank[0], own_bank[0], left_bank[1], own_bank[1]]
+        moving = {a: operand("dy%d" % a, H, 0, 128) for a in range(3)}
         stationary = {a: operand("x8_%d" % a, D, 64, 192) for a in (1, 2)}
 
         def interleave(copy, raw, lo, hi, op, at):
@@ -122,12 +123,15 @@ def tile_mix_dwsav_none_kernel(tc, x4_words, x4_scales, x8, dy, out):
             for m in blocks:
                 multiply(a, m, last_bank[m], LAST, 0, NARROW, a == 0, False)
 
-        def close(sums, at, stops):
+        def close(a, sums, at, stops):
             for i in range(2):
                 for m in range(2):
-                    multiply(2, m, sums[m], at, i * PART, PART, False, i == 1 and m in stops)
+                    multiply(a, m, sums[m], at, i * PART, PART, False, i == 1 and m in stops)
             for m in range(2, M_TILES):
-                multiply(2, m, sums[m], at, 0, NARROW, False, m in stops)
+                multiply(a, m, sums[m], at, 0, NARROW, False, m in stops)
+
+        def close_pairs(a, banks, at):
+            close(a, [banks[m // 2][:, m % 2 * NARROW :] for m in range(M_TILES)], at, (1, 3))
 
         def store(staged, h0, m0, count):
             nc.sync.dma_start(
@@ -135,10 +139,8 @@ def tile_mix_dwsav_none_kernel(tc, x4_words, x4_scales, x8, dy, out):
                 in_=staged[:, m0 * NARROW : (m0 + count) * NARROW].rearrange("p (i h) -> p i h", i=count),
             )
 
-        def empty_pairs(staged, banks, h0):
-            for pair in range(2):
-                scalar(out=staged[:, pair * BANK : (pair + 1) * BANK], in_=banks[pair][:])
-            store(staged, h0, 0, M_TILES)
+        def empty_pair(staged, banks, pair):
+            scalar(out=staged[:, pair * BANK : (pair + 1) * BANK], in_=banks[pair][:])
 
         dy0 = load_dy(0, 0, H)
         x4_rows = keep.tile([SCALE_ROWS, QUADRANTS * D], U8, name="x4_rows", align_bytes=ALIGN)
@@ -159,9 +161,10 @@ def tile_mix_dwsav_none_kernel(tc, x4_words, x4_scales, x8, dy, out):
         dy1_last = load_dy(1, LAST, H)
         dy2_last = load_dy(2, LAST, H)
 
-        for lo in (0, MID):
-            copy_dy(vector, dy0, 0, 0, lo, lo + NARROW)
-            copy_dy(scalar, dy0, 0, 0, lo + NARROW, lo + LEFT)
+        copy_dy(vector, dy0, 0, 0, 0, V_WIDE)
+        copy_dy(scalar, dy0, 0, 0, V_WIDE, LEFT)
+        copy_dy(vector, dy0, 0, 0, MID, LAST)
+        copy_dy(scalar, dy0, 0, 0, LAST, H)
         quantize_dy(0, 0, LEFT)
         for q in range(QUADRANTS):
             vector(
@@ -172,46 +175,55 @@ def tile_mix_dwsav_none_kernel(tc, x4_words, x4_scales, x8, dy, out):
         for half in range(2):
             left_pass(0, half, True, False)
         paired_pass(0, mid_bank, MID, True, False)
-        last_pass(0, range(2))
+        last_pass(0, (1, 3))
 
         for a in (2, 1):
             rows = x_raw[:, (a - 1) * PACK : a * PACK, :]
-            interleave(vector, rows, 0, D // 2, stationary[a], 0)
-            interleave(scalar, rows, D // 2, D, stationary[a], 0)
+            interleave(vector, rows, 0, V_WIDE, stationary[a], 0)
+            interleave(scalar, rows, V_WIDE, D, stationary[a], 0)
         quantize(stationary[2], E4M3X4, 0, D)
+        quantize(stationary[1], E4M3X4, 0, D // 2)
         copy_dy(vector, dy2_left, 2, 0, 0, NARROW)
-        copy_dy(scalar, dy2_left, 2, 0, NARROW, LEFT)
-        quantize(stationary[1], E4M3X4, 0, D)
+        copy_dy(vector, dy2_left, 2, 0, NARROW, V_WIDE)
+        copy_dy(scalar, dy2_left, 2, 0, V_WIDE, LEFT)
+        quantize_dy(2, 0, NARROW)
+        quantize(stationary[1], E4M3X4, D // 2, D // 2)
+        quantize_dy(2, NARROW, NARROW)
         for half in range(2):
-            quantize_dy(2, half * NARROW, NARROW)
             left_pass(2, half, False, False)
 
         copy_dy(vector, dy1_left, 1, 0, 0, V_FIRST)
         copy_dy(scalar, dy1_left, 1, 0, V_FIRST, NARROW)
-        copy_dy(vector, dy1_left, 1, 0, NARROW, LEFT - V_FIRST)
-        copy_dy(scalar, dy1_left, 1, 0, LEFT - V_FIRST, LEFT)
+        copy_dy(vector, dy1_left, 1, 0, NARROW, NARROW + PART)
+        copy_dy(scalar, dy1_left, 1, 0, NARROW + PART, LEFT)
         copy_dy(scalar, dy1_mid, 1, MID, PART, NARROW)
-        quantize_dy(1, 0, NARROW)
+        for i in range(2):
+            quantize_dy(1, i * PART, PART)
         copy_dy(vector, dy1_mid, 1, MID, 0, PART)
         quantize_dy(1, NARROW, NARROW)
+        close_pairs(1, left_bank, 0)
+        left_pass(1, 1, False, True)
         for half in range(2):
-            left_pass(1, half, False, True)
-            empty_pairs(left[half], left_bank[2 * half : 2 * half + 2], half * NARROW)
+            for pair in range(2):
+                empty_pair(left[half], left_bank[2 * half :], pair)
+            store(left[half], half * NARROW, 0, M_TILES)
 
         quantize_dy(1, MID, NARROW)
         paired_pass(1, mid_bank, MID, False, False)
         prepare_alone(dy2_mid, 2, MID)
-        close([mid_bank[m // 2][:, m % 2 * NARROW :] for m in range(M_TILES)], MID, (1, 3))
-        empty_pairs(mid, mid_bank, MID)
+        close_pairs(2, mid_bank, MID)
+        for pair in range(2):
+            empty_pair(mid, mid_bank, pair)
+            store(mid, MID, 2 * pair, 2)
 
-        last_pass(0, range(2, M_TILES))
+        last_pass(0, (0, 2))
         prepare_alone(dy1_last, 1, LAST)
         last_pass(1, range(M_TILES))
         prepare_alone(dy2_last, 2, LAST)
-        close(last_bank, LAST, range(M_TILES))
+        close(2, last_bank, LAST, range(M_TILES))
 
         for m in range(M_TILES):
-            copy = scalar if m % 2 else vector
+            copy = vector if m % 2 else scalar
             copy(out=last[:, m * NARROW : (m + 1) * NARROW], in_=last_bank[m][:, :NARROW])
             if m % 2:
                 store(last, LAST, m - 1, 2)

from contextlib import ExitStack

import concourse.mybir as mybir

F32 = mybir.dt.float32
BF16 = mybir.dt.bfloat16
I32 = mybir.dt.int32
U32 = mybir.dt.uint32
U8 = mybir.dt.uint8
E4M3X4 = mybir.dt.float8_e4m3fn_x4
E5M2X4 = mybir.dt.float8_e5m2_x4
E2M1X4 = mybir.dt.float4_e2m1fn_x4

T, D, H = 1536, 512, 1024
P = 128
PACK = 4
K_PASS = P * PACK
M_TILE = 128
M_TILES = D // M_TILE
BANK = 512
LEFT = BANK
NARROW = LEFT // 2
MID = LEFT
LAST = MID + NARROW
PART = NARROW // 2
QUADRANTS, QUADRANT, SCALE_ROWS = 4, 32, 4
RUN = 4

ALIGN = 256

V_WIDE = 288
V_FIRST = 160

FLOPS = 2 * T * D * H


def tile_mix_dwsav_none_kernel(tc, x4_words, x4_scales, x8, dy, out):
    nc = tc.nc
    with ExitStack() as ctx:
        keep = ctx.enter_context(tc.tile_pool(name="keep", bufs=1))
        psum = ctx.enter_context(tc.psum_pool(name="psum", bufs=1))
        ctx.enter_context(tc.manual_schedule())
        vector, scalar = nc.vector.tensor_copy, nc.scalar.copy

        x4_codes = keep.tile([P, 2 * D], U8, name="x4_codes", align_bytes=ALIGN)
        x4_plane = keep.tile([P, D], U8, name="x4_plane", align_bytes=ALIGN)
        nc.vector.memset(x4_plane[:].bitcast(I32), 0)

        def load_dy(a, lo, hi):
            raw = keep.tile([P, PACK, hi - lo], F32, name="raw_dy%d_%d" % (a, lo), align_bytes=ALIGN)
            rows = dy[a * K_PASS : (a + 1) * K_PASS, lo:hi]
            nc.sync.dma_start(out=raw[:], in_=rows.rearrange("(p j) w -> p j w", j=PACK))
            return raw

        def operand(name, width, codes_at, plane_at):
            grouped = keep.tile([P, PACK * width], BF16, name="grouped_" + name, align_bytes=ALIGN)
            codes = keep.tile([P, width + ALIGN // 4], U32, name="codes_" + name, align_bytes=ALIGN)
            plane = keep.tile([P, width + ALIGN], U8, name="plane_" + name, align_bytes=ALIGN)
            return grouped, codes[:, codes_at // 4 : codes_at // 4 + width], plane[:, plane_at : plane_at + width]

        left = [keep.tile([M_TILE, M_TILES * NARROW], F32, name="left%d" % i, align_bytes=ALIGN) for i in range(2)]
        mid = keep.tile([M_TILE, M_TILES * NARROW], F32, name="mid", align_bytes=ALIGN)
        last = keep.tile([M_TILE, M_TILES * NARROW], F32, name="last", align_bytes=ALIGN)
        left_bank = [psum.tile([M_TILE, BANK], F32, name="left_bank%d" % m) for m in range(M_TILES)]
        mid_bank = [psum.tile([M_TILE, BANK], F32, name="mid_bank%d" % pair) for pair in range(2)]
        own_bank = [psum.tile([M_TILE, BANK], F32, name="own_bank%d" % i) for i in range(2)]
        last_bank = [left_bank[0], own_bank[0], left_bank[1], own_bank[1]]
        moving = {a: operand("dy%d" % a, H, 0, 128) for a in range(3)}
        stationary = {a: operand("x8_%d" % a, D, 64, 192) for a in (1, 2)}

        def interleave(copy, raw, lo, hi, op, at):
            copy(
                out=op[0][:, PACK * (at + lo) : PACK * (at + hi)].rearrange("p (c i j) -> p c j i", i=RUN, j=PACK),
                in_=raw[:, :, lo:hi].rearrange("p j (c i) -> p c j i", i=RUN),
            )

        def quantize(op, fmt, at, width):
            nc.vector.quantize_mx(
                out=op[1][:, at : at + width].bitcast(fmt),
                scales=op[2][:, at : at + width],
                in_=op[0][:, PACK * at : PACK * (at + width)],
            )

        def copy_dy(copy, raw, a, at, lo, hi):
            interleave(copy, raw, lo, hi, moving[a], at)

        def quantize_dy(a, at, width):
            quantize(moving[a], E5M2X4, at, width)

        def prepare_alone(raw, a, at):
            for i in range(2):
                copy_dy(vector, raw, a, at, i * PART, (i + 1) * PART)
            for i in range(2):
                quantize_dy(a, at + i * PART, PART)

        def multiply(a, m, bank, at, lo, width, start, stop):
            cols = slice(m * M_TILE, (m + 1) * M_TILE)
            if a == 0:
                lhsT = x4_codes[:, 2 * m * M_TILE : 2 * (m + 1) * M_TILE].bitcast(E2M1X4)
                lhsT_scale = x4_plane[:, cols]
            else:
                lhsT = stationary[a][1][:, cols].bitcast(E4M3X4)
                lhsT_scale = stationary[a][2][:, cols]
            nc.tensor.matmul_mx(
                out=bank[:, lo : lo + width],
                lhsT=lhsT,
                lhsT_scale=lhsT_scale,
                rhs=moving[a][1][:, at + lo : at + lo + width].bitcast(E5M2X4),
                rhs_scale=moving[a][2][:, at + lo : at + lo + width],
                start=start,
                stop=stop,
            )

        def paired_pass(a, banks, at, first, closing):
            for m in range(M_TILES):
                odd = m % 2
                multiply(a, m, banks[m // 2][:, odd * NARROW :], at, 0, NARROW, first and not odd, closing and odd == 1)

        def left_pass(a, half, first, closing):
            paired_pass(a, left_bank[2 * half : 2 * half + 2], half * NARROW, first, closing)

        def last_pass(a, blocks):
            for m in blocks:
                multiply(a, m, last_bank[m], LAST, 0, NARROW, a == 0, False)

        def close(a, sums, at, stops):
            for i in range(2):
                for m in range(2):
                    multiply(a, m, sums[m], at, i * PART, PART, False, i == 1 and m in stops)
            for m in range(2, M_TILES):
                multiply(a, m, sums[m], at, 0, NARROW, False, m in stops)

        def close_pairs(a, banks, at):
            close(a, [banks[m // 2][:, m % 2 * NARROW :] for m in range(M_TILES)], at, (1, 3))

        def store(staged, h0, m0, count):
            nc.sync.dma_start(
                out=out[m0 * M_TILE : (m0 + count) * M_TILE, h0 : h0 + NARROW].rearrange("(i p) h -> p i h", i=count),
                in_=staged[:, m0 * NARROW : (m0 + count) * NARROW].rearrange("p (i h) -> p i h", i=count),
            )

        def empty_pair(staged, banks, pair):
            scalar(out=staged[:, pair * BANK : (pair + 1) * BANK], in_=banks[pair][:])

        dy0 = load_dy(0, 0, H)
        x4_rows = keep.tile([SCALE_ROWS, QUADRANTS * D], U8, name="x4_rows", align_bytes=ALIGN)
        nc.sync.dma_start(
            out=x4_rows[:].bitcast(I32).rearrange("r (q n) -> r q n", q=QUADRANTS),
            in_=x4_scales[0].bitcast(I32).rearrange("(q r) n -> r q n", q=QUADRANTS),
        )
        x_raw = keep.tile([P, 2 * PACK, D], F32, name="x_raw", align_bytes=ALIGN)
        nc.sync.dma_start(
            out=x_raw[:].rearrange("p (a j) w -> p a (j w)", a=2),
            in_=x8.rearrange("(a p j) w -> p a (j w)", a=2, j=PACK),
        )
        nc.sync.dma_start(out=x4_codes[:].bitcast(I32), in_=x4_words[0].bitcast(I32))
        dy2_left = load_dy(2, 0, LEFT)
        dy1_left = load_dy(1, 0, LEFT)
        dy1_mid = load_dy(1, MID, LAST)
        dy2_mid = load_dy(2, MID, LAST)
        dy1_last = load_dy(1, LAST, H)
        dy2_last = load_dy(2, LAST, H)

        copy_dy(vector, dy0, 0, 0, 0, V_WIDE)
        copy_dy(scalar, dy0, 0, 0, V_WIDE, LEFT)
        copy_dy(vector, dy0, 0, 0, MID, LAST)
        copy_dy(scalar, dy0, 0, 0, LAST, H)
        quantize_dy(0, 0, LEFT)
        for q in range(QUADRANTS):
            vector(
                out=x4_plane[QUADRANT * q : QUADRANT * q + SCALE_ROWS, :].bitcast(I32),
                in_=x4_rows[:, q * D : (q + 1) * D].bitcast(I32),
            )
        quantize_dy(0, MID, H - MID)
        for half in range(2):
            left_pass(0, half, True, False)
        paired_pass(0, mid_bank, MID, True, False)
        last_pass(0, (1, 3))

        for a in (2, 1):
            rows = x_raw[:, (a - 1) * PACK : a * PACK, :]
            interleave(vector, rows, 0, V_WIDE, stationary[a], 0)
            interleave(scalar, rows, V_WIDE, D, stationary[a], 0)
        quantize(stationary[2], E4M3X4, 0, D)
        quantize(stationary[1], E4M3X4, 0, D // 2)
        copy_dy(vector, dy2_left, 2, 0, 0, NARROW)
        copy_dy(vector, dy2_left, 2, 0, NARROW, V_WIDE)
        copy_dy(scalar, dy2_left, 2, 0, V_WIDE, LEFT)
        quantize_dy(2, 0, NARROW)
        quantize(stationary[1], E4M3X4, D // 2, D // 2)
        quantize_dy(2, NARROW, NARROW)
        for half in range(2):
            left_pass(2, half, False, False)

        copy_dy(vector, dy1_left, 1, 0, 0, V_FIRST)
        copy_dy(scalar, dy1_left, 1, 0, V_FIRST, NARROW)
        copy_dy(vector, dy1_left, 1, 0, NARROW, NARROW + PART)
        copy_dy(scalar, dy1_left, 1, 0, NARROW + PART, LEFT)
        copy_dy(scalar, dy1_mid, 1, MID, PART, NARROW)
        for i in range(2):
            quantize_dy(1, i * PART, PART)
        copy_dy(vector, dy1_mid, 1, MID, 0, PART)
        quantize_dy(1, NARROW, NARROW)
        close_pairs(1, left_bank, 0)
        left_pass(1, 1, False, True)
        for half in range(2):
            for pair in range(2):
                empty_pair(left[half], left_bank[2 * half :], pair)
            store(left[half], half * NARROW, 0, M_TILES)

        quantize_dy(1, MID, NARROW)
        paired_pass(1, mid_bank, MID, False, False)
        prepare_alone(dy2_mid, 2, MID)
        close_pairs(2, mid_bank, MID)
        for pair in range(2):
            empty_pair(mid, mid_bank, pair)
            store(mid, MID, 2 * pair, 2)

        last_pass(0, (0, 2))
        prepare_alone(dy1_last, 1, LAST)
        last_pass(1, range(M_TILES))
        prepare_alone(dy2_last, 2, LAST)
        close(2, last_bank, LAST, range(M_TILES))

        for m in range(M_TILES):
            copy = vector if m % 2 else scalar
            copy(out=last[:, m * NARROW : (m + 1) * NARROW], in_=last_bank[m][:, :NARROW])
            if m % 2:
                store(last, LAST, m - 1, 2)
